import numpy as np
import ml_dtypes


def mxq(x, axis, fmt="e4m3"):
    dtype, down = {"e4m3": (ml_dtypes.float8_e4m3fn, 7), "e5m2": (ml_dtypes.float8_e5m2, 14)}[fmt]
    v = np.moveaxis(np.asarray(x, np.float32).astype(ml_dtypes.bfloat16).astype(np.float64), axis, -1)
    blocks = v.reshape(v.shape[:-1] + (-1, 32))
    amax = np.abs(blocks).max(-1, keepdims=True)
    byte = np.maximum(np.where(amax > 0, np.frexp(amax)[1] - 1 + 127, 0) - down, 1)
    scale = np.exp2(byte - 127.0)
    codes = (blocks / scale).astype(np.float32).astype(dtype).astype(np.float64)
    return np.moveaxis((codes * scale).reshape(v.shape), -1, axis)


WIDE = False


def mx_kscale(k):
    if not WIDE:
        return np.ones(k)
    levels = np.array([24, -24, 12, -12, 0])
    if k % 512:
        return np.exp2(np.random.permutation(np.resize(levels, k // 32))).repeat(32)
    a = np.empty((k // 512, 16))
    for p in range(k // 512):
        a[p, :8] = np.random.permutation(np.resize(levels, 8))
        for g in range(8):
            far = levels[np.abs(levels - a[p, g]) >= 10]
            a[p, g + 8] = far[np.random.randint(len(far))]
    return np.exp2(a.ravel()).repeat(32)


def f64(x):
    return np.asarray(x).astype(np.float64)


def striped(idx):
    return np.tile(idx.reshape(-1, 16).T, (8, 1)).astype(np.uint16)


def unstriped(offs):
    return offs[:16].T.reshape(-1).astype(np.int64)


E2M1 = np.array([0.0, 0.5, 1.0, 1.5, 2.0, 3.0, 4.0, 6.0, -0.0, -0.5, -1.0, -1.5, -2.0, -3.0, -4.0, -6.0])


def pack_weight(w, fmt):
    k, n = w.shape
    w = f64(np.asarray(w, np.float32).astype(ml_dtypes.bfloat16)).reshape(k // 32, 32, n)
    amax = np.abs(w).max(1)
    if fmt == "e4m3":
        byte = np.frexp(amax)[1] - 1 + 127 - 7
    else:
        mant, ex = np.frexp(amax / 6.0)
        byte = np.where(mant > 0.5, ex, ex - 1) + 127
    byte = np.clip(np.where(amax > 0, byte, 1), 1, 254)
    scaled = (w * np.exp2(127.0 - byte)[:, None, :]).reshape(k, n).astype(np.float32)
    by_word = np.ascontiguousarray(scaled.reshape(k // 512, 128, 4, n).transpose(0, 1, 3, 2))
    if fmt == "e4m3":
        words = by_word.astype(ml_dtypes.float8_e4m3fn).view(np.uint8)
    else:
        c = by_word.astype(ml_dtypes.float4_e2m1fn).view(np.uint8) & 0xF
        words = (c[..., 0::2] | (c[..., 1::2] << 4)).reshape(k // 512, 128, 2 * n)
    return np.ascontiguousarray(words), np.ascontiguousarray(byte.astype(np.uint8).reshape(k // 512, 16, n))


def unpack_weight(words, scales, fmt):
    g, _, n = scales.shape
    words = np.ascontiguousarray(words).reshape(g, 128, n, -1)
    if fmt == "e4m3":
        vals = words.view(ml_dtypes.float8_e4m3fn).astype(np.float64)
    else:
        nib = np.empty((g, 128, n, 4), np.uint8)
        nib[..., 0::2] = words & 0xF
        nib[..., 1::2] = words >> 4
        vals = E2M1[nib]
    vals = vals * np.repeat(np.exp2(scales.astype(np.float64) - 127.0), 8, axis=1)[..., None]
    return vals.transpose(0, 1, 3, 2).reshape(g * 512, n)


def sigm(f):
    return 1.0 / (1.0 + np.exp(-np.maximum(f, -700.0)))


K, R, N, T, J = 1024, 512, 256, 4096, 2048


def setup_inputs():
    n = np.random.standard_normal
    s = mx_kscale(K)[:, None]
    u = mx_kscale(R)[:, None]
    p_tab = pack_weight(n((K, T)) * s, "e4m3")
    p_wg = pack_weight(n((K, R)) / np.sqrt(K) / s, "e2m1")
    p_wu = pack_weight(n((K, R)) / np.sqrt(K) / s * u.T, "e2m1")
    p_wd = pack_weight(n((R, N)) / np.sqrt(R) / u, "e4m3")
    return {
        "tab_words": p_tab[0],
        "tab_scales": p_tab[1],
        "wg_words": p_wg[0],
        "wg_scales": p_wg[1],
        "wu_words": p_wu[0],
        "wu_scales": p_wu[1],
        "wd_words": p_wd[0],
        "wd_scales": p_wd[1],
        "rT": (n((N, T))).astype(np.float32),
        "offs": striped(np.random.permutation(T)[:J]),
    }


def reference(tab_words, tab_scales, wg_words, wg_scales, wu_words, wu_scales, wd_words, wd_scales, rT, offs):
    idx = unstriped(offs)
    tab_ = unpack_weight(tab_words, tab_scales, "e4m3")[:, idx]
    wg_ = unpack_weight(wg_words, wg_scales, "e2m1")
    wu_ = unpack_weight(wu_words, wu_scales, "e2m1")
    ga = wg_.T @ tab_
    ub = wu_.T @ tab_
    h = sigm(ga) * ub
    h_ = mxq(h, 0, "e4m3")
    wd_ = unpack_weight(wd_words, wd_scales, "e4m3")
    y = wd_.T @ h_
    return y + f64(rT)[:, idx]

@@ -1,0 +1,197 @@
+from contextlib import ExitStack
+
+import concourse.mybir as mybir
+
+K, R, N, T, J = 1024, 512, 256, 4096, 2048
+FLOPS = 2 * J * (2 * K * R + R * N)
+
+F32 = mybir.dt.float32
+BF16 = mybir.dt.bfloat16
+I32 = mybir.dt.int32
+U32 = mybir.dt.uint32
+U16 = mybir.dt.uint16
+U8 = mybir.dt.uint8
+FP8X4 = mybir.dt.float8_e4m3fn_x4
+FP4X4 = mybir.dt.float4_e2m1fn_x4
+MULT = mybir.AluOpType.mult
+ADD = mybir.AluOpType.add
+SIGMOID = mybir.ActivationFunctionType.Sigmoid
+
+P = 128
+PASSES = K // 512
+QUADS = 4
+GATHER = 512
+SUB = 128
+GROUPS = [512, 512, 512, 256, 256]
+
+
+def tile_list_gmlpt_sigm_resL_kernel(
+    tc, tab_words, tab_scales, wg_words, wg_scales, wu_words, wu_scales, wd_words, wd_scales, rT, offs, out
+):
+    nc = tc.nc
+    with ExitStack() as ctx:
+        keep = ctx.enter_context(tc.tile_pool(name="keep", bufs=1))
+        ring = ctx.enter_context(tc.tile_pool(name="ring", bufs=3))
+        psum = ctx.enter_context(tc.psum_pool(name="psum", bufs=3))
+        psum_y = ctx.enter_context(tc.psum_pool(name="psum_y", bufs=2))
+
+        offsets = keep.tile([P, J // 16], U16, name="offsets")
+        nc.sync.dma_start(offsets[:], offs)
+
+        scale_table = keep.tile([P, T // 4], I32, name="scale_table", tag="slot_a", align_bytes=64)
+        nc.vector.memset(scale_table[:], 0)
+        nc.sync.dma_start(
+            scale_table[0:P:4, :], tab_scales.rearrange("a q t -> (a q) t").bitcast(I32)
+        )
+
+        planes = keep.tile([P, PASSES, J // 4], I32, name="planes", align_bytes=64)
+        w_scale_raw = keep.tile([P, 2 * PASSES, R // 4], I32, name="w_scale_raw", align_bytes=64)
+        wd_plane = keep.tile([P, N // 4], I32, name="wd_plane", align_bytes=64)
+        nc.vector.memset(w_scale_raw[:], 0)
+        nc.vector.memset(wd_plane[:], 0)
+        nc.vector.memset(planes[:], 0)
+
+        word_table = [
+            keep.tile([P, T], I32, name="word_table%d" % a, tag="slot_w%d" % a, align_bytes=64)
+            for a in range(PASSES)
+        ]
+
+        def load_words(a):
+            src = tab_words[a].rearrange("p t i -> p (t i)").bitcast(I32)
+            nc.sync.dma_start(word_table[a][:], src)
+
+        def load_weight_scales(m, scales):
+            for q in range(QUADS):
+                nc.sync.dma_start(
+                    w_scale_raw[32 * q : 32 * q + 4, PASSES * m : PASSES * (m + 1), :],
+                    scales[:, 4 * q : 4 * q + 4, :].bitcast(I32).rearrange("a r n -> r a n"),
+                )
+
+        load_weight_scales(0, wg_scales)
+        load_words(0)
+        w_raw = keep.tile([P, 2 * PASSES, R // 2], I32, name="w_raw", align_bytes=64)
+        for m, words in enumerate((wg_words, wu_words)):
+            nc.sync.dma_start(
+                w_raw[:, PASSES * m : PASSES * (m + 1), :], words.bitcast(I32).rearrange("a p n -> p a n")
+            )
+        load_weight_scales(1, wu_scales)
+        load_words(1)
+
+        wd_codes = keep.tile([P, N], I32, name="wd_codes", align_bytes=64)
+        nc.gpsimd.dma_start(wd_codes[:], wd_words[0].rearrange("p n i -> p (n i)").bitcast(I32))
+        for q in range(QUADS):
+            nc.gpsimd.dma_start(
+                wd_plane[32 * q : 32 * q + 4, :], wd_scales[0, 4 * q : 4 * q + 4, :].bitcast(I32)
+            )
+
+        picked_scales = keep.tile([P, J], U8, name="picked_scales", tag="slot_b", align_bytes=64)
+        nc.vector.tensor_copy(picked_scales[:], scale_table[:].bitcast(U8).indirect(offsets[:]))
+        for a in range(PASSES):
+            for q in range(QUADS):
+                first = 64 * a + 16 * q
+                nc.sync.dma_start(
+                    planes[32 * q : 32 * q + 4, a, :],
+                    picked_scales[first : first + 16 : 4, :].bitcast(I32),
+                )
+
+        picked = [keep.tile([P, J], U32, name="picked%d" % a, align_bytes=64) for a in range(PASSES)]
+
+        res_table = [
+            keep.tile([P, T], F32, name="res_table0", tag="slot_a", align_bytes=64),
+            keep.tile([P, T], F32, name="res_table1", tag="slot_b", align_bytes=64),
+        ]
+        for half in range(2):
+            nc.sync.dma_start(res_table[half][:], rT[half * P : (half + 1) * P, :])
+
+        def listed(j0, width):
+            return offsets[:, j0 // 16 : (j0 + width) // 16]
+
+        def gather_words(a, j0):
+            nc.vector.tensor_copy(
+                picked[a][:, j0 : j0 + GATHER], word_table[a][:].bitcast(U32).indirect(listed(j0, GATHER))
+            )
+
+        gather_words(0, 0)
+
+        w_codes = keep.tile([P, 2 * PASSES, R], U16, name="w_codes", align_bytes=64)
+        w_planes = keep.tile([P, 2 * PASSES, R], U8, name="w_planes", align_bytes=64)
+        nc.vector.tensor_copy(
+            w_codes[:].rearrange("p c (t m) -> p c t m", t=4),
+            w_raw[:].bitcast(U16).rearrange("p c (m t) -> p c t m", t=4),
+        )
+        nc.vector.tensor_copy(
+            w_planes[:].rearrange("p c (t m) -> p c t m", t=4),
+            w_scale_raw[:].bitcast(U8).rearrange("p c (m t) -> p c t m", t=4),
+        )
+
+        h = keep.tile([P, J, 4], BF16, name="h", align_bytes=64)
+        h_codes = keep.tile([P, J], U32, name="h_codes", align_bytes=64)
+        h_plane = keep.tile([P, J], U8, name="h_plane", align_bytes=64)
+        res = [keep.tile([P, J], F32, name="res%d" % half) for half in range(2)]
+
+        def gather_residual(j0):
+            for half in range(2):
+                nc.vector.tensor_copy(
+                    res[half][:, j0 : j0 + GATHER], res_table[half][:].indirect(listed(j0, GATHER))
+                )
+
+        def project(m, j0):
+            acc = psum.tile([P, 4, SUB], F32, name="acc%d" % m)
+            for t in range(4):
+                for a in range(PASSES):
+                    cols = slice(t * P, (t + 1) * P)
+                    nc.tensor.matmul_mx(
+                        out=acc[:, t, :],
+                        lhsT=w_codes[:, PASSES * m + a, cols].bitcast(FP4X4),
+                        lhsT_scale=w_planes[:, PASSES * m + a, cols],
+                        rhs=picked[a][:, j0 : j0 + SUB].bitcast(FP8X4),
+                        rhs_scale=planes[:, a, :].bitcast(U8)[:, j0 : j0 + SUB],
+                        start=(a == 0),
+                        stop=(a == PASSES - 1),
+                    )
+            return acc[:].rearrange("p t n -> p n t")
+
+        def gate(j0):
+            ga = project(0, j0)
+            ub = project(1, j0)
+            sig = ring.tile([P, SUB, 4], F32, name="sig")
+            nc.scalar.activation(sig[:], ga, SIGMOID)
+            nc.vector.tensor_tensor(h[:, j0 : j0 + SUB, :], ub, sig[:], MULT)
+
+        def quantize(j0, width):
+            nc.vector.quantize_mx(
+                out=h_codes[:, j0 : j0 + width].bitcast(FP8X4),
+                scales=h_plane[:, j0 : j0 + width],
+                in_=h[:, j0 : j0 + width, :].rearrange("p n t -> p (n t)"),
+            )
+
+        def down(j0, width):
+            for half in range(2):
+                cols = slice(half * P, (half + 1) * P)
+                y = psum_y.tile([P, width], F32, name="y")
+                nc.tensor.matmul_mx(
+                    out=y[:],
+                    lhsT=wd_codes[:, cols].bitcast(FP8X4),
+                    lhsT_scale=wd_plane[:].bitcast(U8)[:, cols],
+                    rhs=h_codes[:, j0 : j0 + width].bitcast(FP8X4),
+                    rhs_scale=h_plane[:, j0 : j0 + width],
+                    start=True,
+                    stop=True,
+                )
+                result = ring.tile([P, width], F32, name="result")
+                nc.vector.tensor_tensor(result[:], y[:], res[half][:, j0 : j0 + width], ADD)
+                nc.sync.dma_start(out[cols, j0 : j0 + width], result[:])
+
+        j0 = 0
+        for width in GROUPS:
+            if j0 % GATHER == 0:
+                if j0 > 0:
+                    gather_words(0, j0)
+                gather_words(1, j0)
+            for s0 in range(j0, j0 + width, SUB):
+                gate(s0)
+            quantize(j0, width)
+            if j0 % GATHER == 0:
+                gather_residual(j0)
+            down(j0, width)
+            j0 += width

@@ -179,7 +179,18 @@ def tile_list_gmlpt_sigm_resL_kernel(
                     stop=True,
                 )
                 result = ring.tile([P, width], F32, name="result")
-                nc.vector.tensor_tensor(result[:], y[:], res[half][:, j0 : j0 + width], ADD)
+                if j0 + width == J:
+                    nc.vector.tensor_tensor(result[:], y[:], res[half][:, j0 : j0 + width], ADD)
+                else:
+                    y_sb = ring.tile([P, width], F32, name="y_sb")
+                    nc.scalar.copy(y_sb[:], y[:])
+                    for c0 in range(0, width, 256):
+                        nc.gpsimd.tensor_tensor(
+                            result[:, c0 : c0 + 256],
+                            y_sb[:, c0 : c0 + 256],
+                            res[half][:, j0 + c0 : j0 + c0 + 256],
+                            ADD,
+                        )
                 nc.sync.dma_start(out[cols, j0 : j0 + width], result[:])
 
         j0 = 0

@@ -1,6 +1,7 @@
 from contextlib import ExitStack
 
 import concourse.mybir as mybir
+from concourse.masks import make_identity
 
 K, R, N, T, J = 1024, 512, 256, 4096, 2048
 FLOPS = 2 * J * (2 * K * R + R * N)
@@ -21,8 +22,8 @@ P = 128
 PASSES = K // 512
 QUADS = 4
 GATHER = 512
-SUB = 128
-GROUPS = [512, 512, 512, 256, 256]
+PAIR = 2 * P
+GROUPS = [512, 512, 512, 256, 128, 128]
 
 
 def tile_list_gmlpt_sigm_resL_kernel(
@@ -32,50 +33,44 @@ def tile_list_gmlpt_sigm_resL_kernel(
     with ExitStack() as ctx:
         keep = ctx.enter_context(tc.tile_pool(name="keep", bufs=1))
         ring = ctx.enter_context(tc.tile_pool(name="ring", bufs=3))
-        psum = ctx.enter_context(tc.psum_pool(name="psum", bufs=3))
+        psum_gate = ctx.enter_context(tc.psum_pool(name="psum_gate", bufs=2))
+        psum_up = ctx.enter_context(tc.psum_pool(name="psum_up", bufs=3))
+        psum_turn = ctx.enter_context(tc.psum_pool(name="psum_turn", bufs=1))
         psum_y = ctx.enter_context(tc.psum_pool(name="psum_y", bufs=2))
 
         offsets = keep.tile([P, J // 16], U16, name="offsets")
         nc.sync.dma_start(offsets[:], offs)
 
-        scale_table = keep.tile([P, T // 4], I32, name="scale_table", tag="slot_a", align_bytes=64)
-        nc.vector.memset(scale_table[:], 0)
-        nc.sync.dma_start(
-            scale_table[0:P:4, :], tab_scales.rearrange("a q t -> (a q) t").bitcast(I32)
-        )
-
-        planes = keep.tile([P, PASSES, J // 4], I32, name="planes", align_bytes=64)
-        w_scale_raw = keep.tile([P, 2 * PASSES, R // 4], I32, name="w_scale_raw", align_bytes=64)
+        scale_table = keep.tile([P, T // 4], I32, name="scale_table", align_bytes=64)
+        w_planes = keep.tile([P, 2 * PASSES, R // 4], I32, name="w_planes", align_bytes=64)
         wd_plane = keep.tile([P, N // 4], I32, name="wd_plane", align_bytes=64)
-        nc.vector.memset(w_scale_raw[:], 0)
-        nc.vector.memset(wd_plane[:], 0)
-        nc.vector.memset(planes[:], 0)
+        planes = keep.tile([P, PASSES, J // 4], I32, name="planes", align_bytes=64)
+        for tile in (w_planes, wd_plane, planes):
+            nc.vector.memset(tile[:], 0)
 
-        word_table = [
-            keep.tile([P, T], I32, name="word_table%d" % a, tag="slot_w%d" % a, align_bytes=64)
-            for a in range(PASSES)
-        ]
+        word_table = [keep.tile([P, T], I32, name="word_table%d" % a, align_bytes=64) for a in range(PASSES)]
+        w_codes = keep.tile([P, 2 * PASSES, R // 2], I32, name="w_codes", align_bytes=64)
 
         def load_words(a):
-            src = tab_words[a].rearrange("p t i -> p (t i)").bitcast(I32)
-            nc.sync.dma_start(word_table[a][:], src)
+            nc.sync.dma_start(word_table[a][:], tab_words[a].rearrange("p t i -> p (t i)").bitcast(I32))
 
-        def load_weight_scales(m, scales):
-            for q in range(QUADS):
-                nc.sync.dma_start(
-                    w_scale_raw[32 * q : 32 * q + 4, PASSES * m : PASSES * (m + 1), :],
+        def load_weight_scales(queues, m, scales):
+            for q, queue in enumerate(queues):
+                queue.dma_start(
+                    w_planes[32 * q : 32 * q + 4, PASSES * m : PASSES * (m + 1), :],
                     scales[:, 4 * q : 4 * q + 4, :].bitcast(I32).rearrange("a r n -> r a n"),
                 )
 
-        load_weight_scales(0, wg_scales)
+        scale_rows = tab_scales.rearrange("a q t -> (a q) t").bitcast(I32)
+        nc.sync.dma_start(scale_table[:], scale_rows.unsqueeze(1).to_broadcast([32, 4, T // 4]))
         load_words(0)
-        w_raw = keep.tile([P, 2 * PASSES, R // 2], I32, name="w_raw", align_bytes=64)
         for m, words in enumerate((wg_words, wu_words)):
             nc.sync.dma_start(
-                w_raw[:, PASSES * m : PASSES * (m + 1), :], words.bitcast(I32).rearrange("a p n -> p a n")
+                w_codes[:, PASSES * m : PASSES * (m + 1), :], words.bitcast(I32).rearrange("a p n -> p a n")
             )
-        load_weight_scales(1, wu_scales)
         load_words(1)
+        load_weight_scales([nc.gpsimd] * QUADS, 0, wg_scales)
+        load_weight_scales([nc.gpsimd, nc.scalar, nc.scalar, nc.scalar], 1, wu_scales)
 
         wd_codes = keep.tile([P, N], I32, name="wd_codes", align_bytes=64)
         nc.gpsimd.dma_start(wd_codes[:], wd_words[0].rearrange("p n i -> p (n i)").bitcast(I32))
@@ -83,80 +78,74 @@ def tile_list_gmlpt_sigm_resL_kernel(
             nc.gpsimd.dma_start(
                 wd_plane[32 * q : 32 * q + 4, :], wd_scales[0, 4 * q : 4 * q + 4, :].bitcast(I32)
             )
+        identity = keep.tile([P, P], F32, name="identity")
+        make_identity(nc, identity[:])
 
         picked_scales = keep.tile([P, J], U8, name="picked_scales", tag="slot_b", align_bytes=64)
         nc.vector.tensor_copy(picked_scales[:], scale_table[:].bitcast(U8).indirect(offsets[:]))
         for a in range(PASSES):
             for q in range(QUADS):
                 first = 64 * a + 16 * q
-                nc.sync.dma_start(
+                nc.scalar.dma_start(
                     planes[32 * q : 32 * q + 4, a, :],
                     picked_scales[first : first + 16 : 4, :].bitcast(I32),
                 )
 
-        picked = [keep.tile([P, J], U32, name="picked%d" % a, align_bytes=64) for a in range(PASSES)]
-
-        res_table = [
-            keep.tile([P, T], F32, name="res_table0", tag="slot_a", align_bytes=64),
-            keep.tile([P, T], F32, name="res_table1", tag="slot_b", align_bytes=64),
-        ]
+        res_table = keep.tile([P, 2, T], F32, name="res_table", tag="slot_b", align_bytes=64)
         for half in range(2):
-            nc.sync.dma_start(res_table[half][:], rT[half * P : (half + 1) * P, :])
+            nc.sync.dma_start(res_table[:, half, :], rT[half * P : (half + 1) * P, :])
 
-        def listed(j0, width):
-            return offsets[:, j0 // 16 : (j0 + width) // 16]
-
-        def gather_words(a, j0):
-            nc.vector.tensor_copy(
-                picked[a][:, j0 : j0 + GATHER], word_table[a][:].bitcast(U32).indirect(listed(j0, GATHER))
-            )
-
-        gather_words(0, 0)
-
-        w_codes = keep.tile([P, 2 * PASSES, R], U16, name="w_codes", align_bytes=64)
-        w_planes = keep.tile([P, 2 * PASSES, R], U8, name="w_planes", align_bytes=64)
-        nc.vector.tensor_copy(
-            w_codes[:].rearrange("p c (t m) -> p c t m", t=4),
-            w_raw[:].bitcast(U16).rearrange("p c (m t) -> p c t m", t=4),
-        )
-        nc.vector.tensor_copy(
-            w_planes[:].rearrange("p c (t m) -> p c t m", t=4),
-            w_scale_raw[:].bitcast(U8).rearrange("p c (m t) -> p c t m", t=4),
-        )
-
+        picked = [keep.tile([P, J], U32, name="picked%d" % a, align_bytes=64) for a in range(PASSES)]
         h = keep.tile([P, J, 4], BF16, name="h", align_bytes=64)
         h_codes = keep.tile([P, J], U32, name="h_codes", align_bytes=64)
         h_plane = keep.tile([P, J], U8, name="h_plane", align_bytes=64)
         res = [keep.tile([P, J], F32, name="res%d" % half) for half in range(2)]
 
-        def gather_residual(j0):
-            for half in range(2):
+        def listed(j0):
+            return offsets[:, j0 // 16 : (j0 + GATHER) // 16]
+
+        def gather_words(j0):
+            for a in range(PASSES):
                 nc.vector.tensor_copy(
-                    res[half][:, j0 : j0 + GATHER], res_table[half][:].indirect(listed(j0, GATHER))
+                    picked[a][:, j0 : j0 + GATHER], word_table[a][:].bitcast(U32).indirect(listed(j0))
                 )
 
-        def project(m, j0):
-            acc = psum.tile([P, 4, SUB], F32, name="acc%d" % m)
-            for t in range(4):
-                for a in range(PASSES):
-                    cols = slice(t * P, (t + 1) * P)
-                    nc.tensor.matmul_mx(
-                        out=acc[:, t, :],
-                        lhsT=w_codes[:, PASSES * m + a, cols].bitcast(FP4X4),
-                        lhsT_scale=w_planes[:, PASSES * m + a, cols],
-                        rhs=picked[a][:, j0 : j0 + SUB].bitcast(FP8X4),
-                        rhs_scale=planes[:, a, :].bitcast(U8)[:, j0 : j0 + SUB],
-                        start=(a == 0),
-                        stop=(a == PASSES - 1),
-                    )
-            return acc[:].rearrange("p t n -> p n t")
+        def gather_residual(j0):
+            for half in range(2):
+                nc.vector.tensor_copy(res[half][:, j0 : j0 + GATHER], res_table[:, half, :].indirect(listed(j0)))
+
+        def project(pool, m, j0):
+            acc = pool.tile([P, R], F32, name="acc%d" % m)
+            for a in range(PASSES):
+                nc.tensor.matmul_mx(
+                    out=acc[:],
+                    lhsT=picked[a][:, j0 : j0 + P].bitcast(FP8X4),
+                    lhsT_scale=planes[:, a, :].bitcast(U8)[:, j0 : j0 + P],
+                    rhs=w_codes[:, PASSES * m + a, :].bitcast(FP4X4),
+                    rhs_scale=w_planes[:, PASSES * m + a, :].bitcast(U8),
+                    start=(a == 0),
+                    stop=(a == PASSES - 1),
+                )
+            return acc[:].rearrange("j (p u e) -> j u p e", u=2, e=2)
 
         def gate(j0):
-            ga = project(0, j0)
-            ub = project(1, j0)
-            sig = ring.tile([P, SUB, 4], F32, name="sig")
+            ga = project(psum_gate, 0, j0)
+            ub = project(psum_up, 1, j0)
+            sig = ring.tile([P, 2, P, 2], F32, name="sig")
             nc.scalar.activation(sig[:], ga, SIGMOID)
-            nc.vector.tensor_tensor(h[:, j0 : j0 + SUB, :], ub, sig[:], MULT)
+            h_rows = ring.tile([P, 2, P, 2], BF16, name="h_rows", bufs=4)
+            nc.vector.tensor_tensor(h_rows[:], ub, sig[:], MULT)
+            return h_rows[:].rearrange("j u p e -> j (u p e)").bitcast(F32)
+
+        def turn(j0, rows):
+            turned = psum_turn.tile([P, len(rows), 2, P], F32, name="turned")
+            for s in range(len(rows)):
+                for u in range(2):
+                    nc.tensor.transpose(turned[:, s, u, :], rows[s][:, u * P : (u + 1) * P], identity[:])
+            words = h[:, j0 : j0 + len(rows) * P, :].rearrange("p j t -> p (j t)").bitcast(F32)
+            nc.scalar.copy(
+                words.rearrange("p (s j u) -> p s j u", j=P, u=2), turned[:].rearrange("p s u j -> p s j u")
+            )
 
         def quantize(j0, width):
             nc.vector.quantize_mx(
@@ -178,11 +167,11 @@ def tile_list_gmlpt_sigm_resL_kernel(
                     start=True,
                     stop=True,
                 )
-                result = ring.tile([P, width], F32, name="result")
-                if j0 + width == J:
+                result = ring.tile([P, width], F32, name="result", bufs=6)
+                if width == P:
                     nc.vector.tensor_tensor(result[:], y[:], res[half][:, j0 : j0 + width], ADD)
                 else:
-                    y_sb = ring.tile([P, width], F32, name="y_sb")
+                    y_sb = ring.tile([P, width], F32, name="y_sb", bufs=8)
                     nc.scalar.copy(y_sb[:], y[:])
                     for c0 in range(0, width, 256):
                         nc.gpsimd.tensor_tensor(
@@ -196,11 +185,9 @@ def tile_list_gmlpt_sigm_resL_kernel(
         j0 = 0
         for width in GROUPS:
             if j0 % GATHER == 0:
-                if j0 > 0:
-                    gather_words(0, j0)
-                gather_words(1, j0)
-            for s0 in range(j0, j0 + width, SUB):
-                gate(s0)
+                gather_words(j0)
+            for s0 in range(j0, j0 + width, PAIR):
+                turn(s0, [gate(s) for s in range(s0, min(s0 + PAIR, j0 + width), P)])
             quantize(j0, width)
             if j0 % GATHER == 0:
                 gather_residual(j0)

@@ -41,22 +41,28 @@ def tile_list_gmlpt_sigm_resL_kernel(
         offsets = keep.tile([P, J // 16], U16, name="offsets")
         nc.sync.dma_start(offsets[:], offs)
 
-        scale_table = keep.tile([P, T // 4], I32, name="scale_table", align_bytes=64)
         w_planes = keep.tile([P, 2 * PASSES, R // 4], I32, name="w_planes", align_bytes=64)
         wd_plane = keep.tile([P, N // 4], I32, name="wd_plane", align_bytes=64)
         planes = keep.tile([P, PASSES, J // 4], I32, name="planes", align_bytes=64)
-        for tile in (w_planes, wd_plane, planes):
+        for tile in (w_planes, planes, wd_plane):
             nc.vector.memset(tile[:], 0)
+
+        identity_stage = keep.tile([P, P], F32, name="identity_stage", tag="word_table1", align_bytes=64)
+        make_identity(nc, identity_stage[:])
+        identity = keep.tile([P, P], F32, name="identity")
+        nc.vector.tensor_copy(identity[:], identity_stage[:])
 
         word_table = [keep.tile([P, T], I32, name="word_table%d" % a, align_bytes=64) for a in range(PASSES)]
         w_codes = keep.tile([P, 2 * PASSES, R // 2], I32, name="w_codes", align_bytes=64)
 
+        scale_table = keep.tile([P, T // 4], I32, name="scale_table", align_bytes=64)
+
         def load_words(a):
             nc.sync.dma_start(word_table[a][:], tab_words[a].rearrange("p t i -> p (t i)").bitcast(I32))
 
-        def load_weight_scales(queues, m, scales):
-            for q, queue in enumerate(queues):
-                queue.dma_start(
+        def load_weight_scales(m, scales):
+            for q in range(QUADS):
+                nc.scalar.dma_start(
                     w_planes[32 * q : 32 * q + 4, PASSES * m : PASSES * (m + 1), :],
                     scales[:, 4 * q : 4 * q + 4, :].bitcast(I32).rearrange("a r n -> r a n"),
                 )
@@ -68,32 +74,26 @@ def tile_list_gmlpt_sigm_resL_kernel(
             nc.sync.dma_start(
                 w_codes[:, PASSES * m : PASSES * (m + 1), :], words.bitcast(I32).rearrange("a p n -> p a n")
             )
-        load_words(1)
-        load_weight_scales([nc.gpsimd] * QUADS, 0, wg_scales)
-        load_weight_scales([nc.gpsimd, nc.scalar, nc.scalar, nc.scalar], 1, wu_scales)
-
         wd_codes = keep.tile([P, N], I32, name="wd_codes", align_bytes=64)
-        nc.gpsimd.dma_start(wd_codes[:], wd_words[0].rearrange("p n i -> p (n i)").bitcast(I32))
+        nc.sync.dma_start(wd_codes[:], wd_words[0].rearrange("p n i -> p (n i)").bitcast(I32))
+        load_words(1)
+        load_weight_scales(0, wg_scales)
+        load_weight_scales(1, wu_scales)
+
         for q in range(QUADS):
             nc.gpsimd.dma_start(
                 wd_plane[32 * q : 32 * q + 4, :], wd_scales[0, 4 * q : 4 * q + 4, :].bitcast(I32)
             )
-        identity = keep.tile([P, P], F32, name="identity")
-        make_identity(nc, identity[:])
 
         picked_scales = keep.tile([P, J], U8, name="picked_scales", tag="slot_b", align_bytes=64)
         nc.vector.tensor_copy(picked_scales[:], scale_table[:].bitcast(U8).indirect(offsets[:]))
         for a in range(PASSES):
             for q in range(QUADS):
                 first = 64 * a + 16 * q
-                nc.scalar.dma_start(
+                nc.sync.dma_start(
                     planes[32 * q : 32 * q + 4, a, :],
                     picked_scales[first : first + 16 : 4, :].bitcast(I32),
                 )
-
-        res_table = keep.tile([P, 2, T], F32, name="res_table", tag="slot_b", align_bytes=64)
-        for half in range(2):
-            nc.sync.dma_start(res_table[:, half, :], rT[half * P : (half + 1) * P, :])
 
         picked = [keep.tile([P, J], U32, name="picked%d" % a, align_bytes=64) for a in range(PASSES)]
         h = keep.tile([P, J, 4], BF16, name="h", align_bytes=64)
@@ -104,15 +104,23 @@ def tile_list_gmlpt_sigm_resL_kernel(
         def listed(j0):
             return offsets[:, j0 // 16 : (j0 + GATHER) // 16]
 
-        def gather_words(j0):
-            for a in range(PASSES):
-                nc.vector.tensor_copy(
-                    picked[a][:, j0 : j0 + GATHER], word_table[a][:].bitcast(U32).indirect(listed(j0))
-                )
+        nc.vector.tensor_copy(picked[0][:], word_table[0][:].bitcast(U32).indirect(offsets[:]))
+
+        def gather_last_pass(j0):
+            nc.vector.tensor_copy(
+                picked[1][:, j0 : j0 + GATHER], word_table[1][:].bitcast(U32).indirect(listed(j0))
+            )
+
+        res_table = [
+            keep.tile([P, T], F32, name="res_table0", tag="scale_table", align_bytes=64),
+            keep.tile([P, T], F32, name="res_table1", tag="slot_b", align_bytes=64),
+        ]
+        for half in range(2):
+            nc.sync.dma_start(res_table[half][:], rT[half * P : (half + 1) * P, :])
 
         def gather_residual(j0):
             for half in range(2):
-                nc.vector.tensor_copy(res[half][:, j0 : j0 + GATHER], res_table[:, half, :].indirect(listed(j0)))
+                nc.vector.tensor_copy(res[half][:, j0 : j0 + GATHER], res_table[half][:].indirect(listed(j0)))
 
         def project(pool, m, j0):
             acc = pool.tile([P, R], F32, name="acc%d" % m)
@@ -168,24 +176,13 @@ def tile_list_gmlpt_sigm_resL_kernel(
                     stop=True,
                 )
                 result = ring.tile([P, width], F32, name="result", bufs=6)
-                if width == P:
-                    nc.vector.tensor_tensor(result[:], y[:], res[half][:, j0 : j0 + width], ADD)
-                else:
-                    y_sb = ring.tile([P, width], F32, name="y_sb", bufs=8)
-                    nc.scalar.copy(y_sb[:], y[:])
-                    for c0 in range(0, width, 256):
-                        nc.gpsimd.tensor_tensor(
-                            result[:, c0 : c0 + 256],
-                            y_sb[:, c0 : c0 + 256],
-                            res[half][:, j0 + c0 : j0 + c0 + 256],
-                            ADD,
-                        )
+                nc.vector.tensor_tensor(result[:], y[:], res[half][:, j0 : j0 + width], ADD)
                 nc.sync.dma_start(out[cols, j0 : j0 + width], result[:])
 
         j0 = 0
         for width in GROUPS:
             if j0 % GATHER == 0:
-                gather_words(j0)
+                gather_last_pass(j0)
             for s0 in range(j0, j0 + width, PAIR):
                 turn(s0, [gate(s) for s in range(s0, min(s0 + PAIR, j0 + width), P)])
             quantize(j0, width)

@@ -41,96 +41,87 @@ def tile_list_gmlpt_sigm_resL_kernel(
         offsets = keep.tile([P, J // 16], U16, name="offsets")
         nc.sync.dma_start(offsets[:], offs)
 
-        w_planes = keep.tile([P, 2 * PASSES, R // 4], I32, name="w_planes", align_bytes=64)
+        w_planes = [keep.tile([P, PASSES, R // 4], I32, name="w_plane%d" % m, align_bytes=64) for m in range(2)]
         wd_plane = keep.tile([P, N // 4], I32, name="wd_plane", align_bytes=64)
         planes = keep.tile([P, PASSES, J // 4], I32, name="planes", align_bytes=64)
-        for tile in (w_planes, planes, wd_plane):
+        for tile in (w_planes[0], w_planes[1], wd_plane, planes):
             nc.vector.memset(tile[:], 0)
 
-        identity_stage = keep.tile([P, P], F32, name="identity_stage", tag="word_table1", align_bytes=64)
-        make_identity(nc, identity_stage[:])
         identity = keep.tile([P, P], F32, name="identity")
-        nc.vector.tensor_copy(identity[:], identity_stage[:])
+        make_identity(nc, identity[:])
 
         word_table = [keep.tile([P, T], I32, name="word_table%d" % a, align_bytes=64) for a in range(PASSES)]
-        w_codes = keep.tile([P, 2 * PASSES, R // 2], I32, name="w_codes", align_bytes=64)
-
+        w_codes = [
+            [keep.tile([P, R // 2], I32, name="w_codes%d%d" % (m, a), align_bytes=64) for a in range(PASSES)]
+            for m in range(2)
+        ]
         scale_table = keep.tile([P, T // 4], I32, name="scale_table", align_bytes=64)
 
-        def load_words(a):
-            nc.sync.dma_start(word_table[a][:], tab_words[a].rearrange("p t i -> p (t i)").bitcast(I32))
+        def pass_rows(rows, a):
+            return rows.bitcast(I32).rearrange("(i a e) c -> a i e c", a=PASSES, e=8)[a]
 
-        def load_weight_scales(m, scales):
-            for q in range(QUADS):
-                nc.scalar.dma_start(
-                    w_planes[32 * q : 32 * q + 4, PASSES * m : PASSES * (m + 1), :],
-                    scales[:, 4 * q : 4 * q + 4, :].bitcast(I32).rearrange("a r n -> r a n"),
-                )
-
-        scale_rows = tab_scales.rearrange("a q t -> (a q) t").bitcast(I32)
+        table_rows = tab_words.rearrange("g p t i -> (g p) (t i)")
+        scale_rows = tab_scales.rearrange("g q t -> (g q) t").bitcast(I32)
         nc.sync.dma_start(scale_table[:], scale_rows.unsqueeze(1).to_broadcast([32, 4, T // 4]))
-        load_words(0)
-        for m, words in enumerate((wg_words, wu_words)):
-            nc.sync.dma_start(
-                w_codes[:, PASSES * m : PASSES * (m + 1), :], words.bitcast(I32).rearrange("a p n -> p a n")
-            )
+        nc.sync.dma_start(word_table[0][:], pass_rows(table_rows, 0))
+        nc.sync.dma_start(word_table[1][:], pass_rows(table_rows, 1))
         wd_codes = keep.tile([P, N], I32, name="wd_codes", align_bytes=64)
         nc.sync.dma_start(wd_codes[:], wd_words[0].rearrange("p n i -> p (n i)").bitcast(I32))
-        load_words(1)
-        load_weight_scales(0, wg_scales)
-        load_weight_scales(1, wu_scales)
+        res_table = [keep.tile([P, T], F32, name="res_table%d" % half, align_bytes=64) for half in range(2)]
+        for half in range(2):
+            nc.sync.dma_start(res_table[half][:], rT[half * P : (half + 1) * P, :])
 
+        for m, scales in enumerate((wg_scales, wu_scales)):
+            blocks = scales.rearrange("g q n -> (g q) n").bitcast(I32).rearrange("(i a) n -> i a n", a=PASSES)
+            for q in range(QUADS):
+                nc.scalar.dma_start(w_planes[m][32 * q : 32 * q + 4, :, :], blocks[4 * q : 4 * q + 4, :, :])
+        for a in range(PASSES):
+            for m, words in enumerate((wg_words, wu_words)):
+                nc.scalar.dma_start(w_codes[m][a][:], pass_rows(words.rearrange("g p n -> (g p) n"), a))
         for q in range(QUADS):
             nc.gpsimd.dma_start(
                 wd_plane[32 * q : 32 * q + 4, :], wd_scales[0, 4 * q : 4 * q + 4, :].bitcast(I32)
             )
 
-        picked_scales = keep.tile([P, J], U8, name="picked_scales", tag="slot_b", align_bytes=64)
+        picked_scales = keep.tile([P, J], U8, name="picked_scales", align_bytes=64)
         nc.vector.tensor_copy(picked_scales[:], scale_table[:].bitcast(U8).indirect(offsets[:]))
-        for a in range(PASSES):
-            for q in range(QUADS):
-                first = 64 * a + 16 * q
-                nc.sync.dma_start(
-                    planes[32 * q : 32 * q + 4, a, :],
-                    picked_scales[first : first + 16 : 4, :].bitcast(I32),
-                )
-
-        picked = [keep.tile([P, J], U32, name="picked%d" % a, align_bytes=64) for a in range(PASSES)]
-        h = keep.tile([P, J, 4], BF16, name="h", align_bytes=64)
-        h_codes = keep.tile([P, J], U32, name="h_codes", align_bytes=64)
-        h_plane = keep.tile([P, J], U8, name="h_plane", align_bytes=64)
-        res = [keep.tile([P, J], F32, name="res%d" % half) for half in range(2)]
-
-        def listed(j0):
-            return offsets[:, j0 // 16 : (j0 + GATHER) // 16]
-
-        nc.vector.tensor_copy(picked[0][:], word_table[0][:].bitcast(U32).indirect(offsets[:]))
-
-        def gather_last_pass(j0):
-            nc.vector.tensor_copy(
-                picked[1][:, j0 : j0 + GATHER], word_table[1][:].bitcast(U32).indirect(listed(j0))
+        for q in range(QUADS):
+            nc.scalar.dma_start(
+                planes[32 * q : 32 * q + 4, :, :], picked_scales[32 * q : 32 * q + 32 : 4, :].bitcast(I32)
             )
 
-        res_table = [
-            keep.tile([P, T], F32, name="res_table0", tag="scale_table", align_bytes=64),
-            keep.tile([P, T], F32, name="res_table1", tag="slot_b", align_bytes=64),
-        ]
-        for half in range(2):
-            nc.sync.dma_start(res_table[half][:], rT[half * P : (half + 1) * P, :])
+        picked_first = keep.tile([P, J], U32, name="picked_first", align_bytes=64)
+        h_codes = keep.tile([P, J], U32, name="h_codes", align_bytes=64)
+        h_plane = keep.tile([P, J], U8, name="h_plane", align_bytes=64)
 
-        def gather_residual(j0):
-            for half in range(2):
-                nc.vector.tensor_copy(res[half][:, j0 : j0 + GATHER], res_table[half][:].indirect(listed(j0)))
+        def listed(j0, width):
+            return offsets[:, j0 // 16 : (j0 + width) // 16]
+
+        for j0, width in ((0, GATHER), (GATHER, J - GATHER)):
+            nc.vector.tensor_copy(
+                picked_first[:, j0 : j0 + width], word_table[0][:].bitcast(U32).indirect(listed(j0, width))
+            )
+
+        picked_last = {}
+
+        def gather_last_pass(j0):
+            picked_last[j0] = ring.tile([P, GATHER], U32, name="picked_last", bufs=2, align_bytes=64)
+            nc.vector.tensor_copy(picked_last[j0][:], word_table[1][:].bitcast(U32).indirect(listed(j0, GATHER)))
+
+        def picked(a, j0):
+            if a == 0:
+                return picked_first[:, j0 : j0 + P]
+            return picked_last[j0 - j0 % GATHER][:, j0 % GATHER : j0 % GATHER + P]
 
         def project(pool, m, j0):
             acc = pool.tile([P, R], F32, name="acc%d" % m)
             for a in range(PASSES):
                 nc.tensor.matmul_mx(
                     out=acc[:],
-                    lhsT=picked[a][:, j0 : j0 + P].bitcast(FP8X4),
+                    lhsT=picked(a, j0).bitcast(FP8X4),
                     lhsT_scale=planes[:, a, :].bitcast(U8)[:, j0 : j0 + P],
-                    rhs=w_codes[:, PASSES * m + a, :].bitcast(FP4X4),
-                    rhs_scale=w_planes[:, PASSES * m + a, :].bitcast(U8),
+                    rhs=w_codes[m][a][:].bitcast(FP4X4),
+                    rhs_scale=w_planes[m][:, a, :].bitcast(U8),
                     start=(a == 0),
                     stop=(a == PASSES - 1),
                 )
@@ -145,7 +136,7 @@ def tile_list_gmlpt_sigm_resL_kernel(
             nc.vector.tensor_tensor(h_rows[:], ub, sig[:], MULT)
             return h_rows[:].rearrange("j u p e -> j (u p e)").bitcast(F32)
 
-        def turn(j0, rows):
+        def turn(h, j0, rows):
             turned = psum_turn.tile([P, len(rows), 2, P], F32, name="turned")
             for s in range(len(rows)):
                 for u in range(2):
@@ -155,11 +146,11 @@ def tile_list_gmlpt_sigm_resL_kernel(
                 words.rearrange("p (s j u) -> p s j u", j=P, u=2), turned[:].rearrange("p s u j -> p s j u")
             )
 
-        def quantize(j0, width):
+        def quantize(h, j0, width):
             nc.vector.quantize_mx(
                 out=h_codes[:, j0 : j0 + width].bitcast(FP8X4),
                 scales=h_plane[:, j0 : j0 + width],
-                in_=h[:, j0 : j0 + width, :].rearrange("p n t -> p (n t)"),
+                in_=h[:].rearrange("p n t -> p (n t)"),
             )
 
         def down(j0, width):
@@ -175,18 +166,19 @@ def tile_list_gmlpt_sigm_resL_kernel(
                     start=True,
                     stop=True,
                 )
+                y_out = ring.tile([P, width], F32, name="y_out", bufs=4)
+                nc.scalar.copy(y_out[:], y[:])
                 result = ring.tile([P, width], F32, name="result", bufs=6)
-                nc.vector.tensor_tensor(result[:], y[:], res[half][:, j0 : j0 + width], ADD)
+                nc.vector.tensor_tensor(result[:], res_table[half][:].indirect(listed(j0, width)), y_out[:], ADD)
                 nc.sync.dma_start(out[cols, j0 : j0 + width], result[:])
 
         j0 = 0
         for width in GROUPS:
             if j0 % GATHER == 0:
                 gather_last_pass(j0)
+            h = ring.tile([P, width, 4], BF16, name="h", align_bytes=64)
             for s0 in range(j0, j0 + width, PAIR):
-                turn(s0, [gate(s) for s in range(s0, min(s0 + PAIR, j0 + width), P)])
-            quantize(j0, width)
-            if j0 % GATHER == 0:
-                gather_residual(j0)
+                turn(h, s0 - j0, [gate(s) for s in range(s0, min(s0 + PAIR, j0 + width), P)])
+            quantize(h, j0, width)
             down(j0, width)
             j0 += width

@@ -22,8 +22,7 @@ P = 128
 PASSES = K // 512
 QUADS = 4
 GATHER = 512
-PAIR = 2 * P
-GROUPS = [512, 512, 512, 256, 128, 128]
+STEPS = [256] * 7 + [128, 128]
 
 
 def tile_list_gmlpt_sigm_resL_kernel(
@@ -41,54 +40,51 @@ def tile_list_gmlpt_sigm_resL_kernel(
         offsets = keep.tile([P, J // 16], U16, name="offsets")
         nc.sync.dma_start(offsets[:], offs)
 
+        scale_table = keep.tile([P, T // 4], I32, name="scale_table", align_bytes=64)
         w_planes = [keep.tile([P, PASSES, R // 4], I32, name="w_plane%d" % m, align_bytes=64) for m in range(2)]
         wd_plane = keep.tile([P, N // 4], I32, name="wd_plane", align_bytes=64)
         planes = keep.tile([P, PASSES, J // 4], I32, name="planes", align_bytes=64)
-        for tile in (w_planes[0], w_planes[1], wd_plane, planes):
+        for tile in (scale_table, wd_plane, planes):
             nc.vector.memset(tile[:], 0)
+        for tile in w_planes:
+            nc.gpsimd.memset(tile[:], 0)
+
+        word_table = [keep.tile([P, T], I32, name="word_table%d" % a, align_bytes=64) for a in range(PASSES)]
+        w_codes = [keep.tile([P, PASSES, R // 2], I32, name="w_codes%d" % m, align_bytes=64) for m in range(2)]
+        for m, words in enumerate((wg_words, wu_words)):
+            nc.sync.dma_start(w_codes[m][:], words.bitcast(I32).rearrange("a p n -> p a n"))
+        nc.sync.dma_start(scale_table[0:P:4, :], tab_scales.bitcast(I32).rearrange("a q t -> q a t"))
+        for a in range(PASSES):
+            nc.sync.dma_start(word_table[a][:], tab_words[a].rearrange("p t i -> p (t i)").bitcast(I32))
+
+        for m, scales in enumerate((wg_scales, wu_scales)):
+            for q in range(QUADS):
+                queue = nc.scalar if m == 0 and q < 3 else nc.gpsimd
+                queue.dma_start(
+                    w_planes[m][32 * q : 32 * q + 4, :, :],
+                    scales[:, 4 * q : 4 * q + 4, :].bitcast(I32).rearrange("a r n -> r a n"),
+                )
 
         identity = keep.tile([P, P], F32, name="identity")
         make_identity(nc, identity[:])
 
-        word_table = [keep.tile([P, T], I32, name="word_table%d" % a, align_bytes=64) for a in range(PASSES)]
-        w_codes = [
-            [keep.tile([P, R // 2], I32, name="w_codes%d%d" % (m, a), align_bytes=64) for a in range(PASSES)]
-            for m in range(2)
-        ]
-        scale_table = keep.tile([P, T // 4], I32, name="scale_table", align_bytes=64)
-
-        def pass_rows(rows, a):
-            return rows.bitcast(I32).rearrange("(i a e) c -> a i e c", a=PASSES, e=8)[a]
-
-        table_rows = tab_words.rearrange("g p t i -> (g p) (t i)")
-        scale_rows = tab_scales.rearrange("g q t -> (g q) t").bitcast(I32)
-        nc.sync.dma_start(scale_table[:], scale_rows.unsqueeze(1).to_broadcast([32, 4, T // 4]))
-        nc.sync.dma_start(word_table[0][:], pass_rows(table_rows, 0))
-        nc.sync.dma_start(word_table[1][:], pass_rows(table_rows, 1))
-        wd_codes = keep.tile([P, N], I32, name="wd_codes", align_bytes=64)
-        nc.sync.dma_start(wd_codes[:], wd_words[0].rearrange("p n i -> p (n i)").bitcast(I32))
-        res_table = [keep.tile([P, T], F32, name="res_table%d" % half, align_bytes=64) for half in range(2)]
-        for half in range(2):
-            nc.sync.dma_start(res_table[half][:], rT[half * P : (half + 1) * P, :])
-
-        for m, scales in enumerate((wg_scales, wu_scales)):
-            blocks = scales.rearrange("g q n -> (g q) n").bitcast(I32).rearrange("(i a) n -> i a n", a=PASSES)
-            for q in range(QUADS):
-                nc.scalar.dma_start(w_planes[m][32 * q : 32 * q + 4, :, :], blocks[4 * q : 4 * q + 4, :, :])
-        for a in range(PASSES):
-            for m, words in enumerate((wg_words, wu_words)):
-                nc.scalar.dma_start(w_codes[m][a][:], pass_rows(words.rearrange("g p n -> (g p) n"), a))
-        for q in range(QUADS):
-            nc.gpsimd.dma_start(
-                wd_plane[32 * q : 32 * q + 4, :], wd_scales[0, 4 * q : 4 * q + 4, :].bitcast(I32)
-            )
-
-        picked_scales = keep.tile([P, J], U8, name="picked_scales", align_bytes=64)
+        picked_scales = keep.tile([P, J], U8, name="picked_scales", tag="scales_then_residual", align_bytes=64)
         nc.vector.tensor_copy(picked_scales[:], scale_table[:].bitcast(U8).indirect(offsets[:]))
         for q in range(QUADS):
             nc.scalar.dma_start(
                 planes[32 * q : 32 * q + 4, :, :], picked_scales[32 * q : 32 * q + 32 : 4, :].bitcast(I32)
             )
+
+        res_table = [
+            keep.tile([P, T], F32, name="res_table0", tag="scales_then_residual", align_bytes=64),
+            keep.tile([P, T], F32, name="res_table1", align_bytes=64),
+        ]
+        wd_codes = keep.tile([P, N], I32, name="wd_codes", align_bytes=64)
+        nc.sync.dma_start(res_table[0][:], rT[:P, :])
+        nc.sync.dma_start(wd_codes[:], wd_words[0].rearrange("p n i -> p (n i)").bitcast(I32))
+        for q in range(QUADS):
+            nc.sync.dma_start(wd_plane[32 * q : 32 * q + 4, :], wd_scales[0, 4 * q : 4 * q + 4, :].bitcast(I32))
+        nc.sync.dma_start(res_table[1][:], rT[P:, :])
 
         picked_first = keep.tile([P, J], U32, name="picked_first", align_bytes=64)
         h_codes = keep.tile([P, J], U32, name="h_codes", align_bytes=64)
@@ -120,7 +116,7 @@ def tile_list_gmlpt_sigm_resL_kernel(
                     out=acc[:],
                     lhsT=picked(a, j0).bitcast(FP8X4),
                     lhsT_scale=planes[:, a, :].bitcast(U8)[:, j0 : j0 + P],
-                    rhs=w_codes[m][a][:].bitcast(FP4X4),
+                    rhs=w_codes[m][:, a, :].bitcast(FP4X4),
                     rhs_scale=w_planes[m][:, a, :].bitcast(U8),
                     start=(a == 0),
                     stop=(a == PASSES - 1),
@@ -132,21 +128,21 @@ def tile_list_gmlpt_sigm_resL_kernel(
             ub = project(psum_up, 1, j0)
             sig = ring.tile([P, 2, P, 2], F32, name="sig")
             nc.scalar.activation(sig[:], ga, SIGMOID)
-            h_rows = ring.tile([P, 2, P, 2], BF16, name="h_rows", bufs=4)
+            h_rows = ring.tile([P, 2, P, 2], BF16, name="h_rows", bufs=6)
             nc.vector.tensor_tensor(h_rows[:], ub, sig[:], MULT)
             return h_rows[:].rearrange("j u p e -> j (u p e)").bitcast(F32)
 
-        def turn(h, j0, rows):
+        def turn(j0, rows):
             turned = psum_turn.tile([P, len(rows), 2, P], F32, name="turned")
             for s in range(len(rows)):
                 for u in range(2):
                     nc.tensor.transpose(turned[:, s, u, :], rows[s][:, u * P : (u + 1) * P], identity[:])
-            words = h[:, j0 : j0 + len(rows) * P, :].rearrange("p j t -> p (j t)").bitcast(F32)
+            width = len(rows) * P
+            h = ring.tile([P, width, 4], BF16, name="h", align_bytes=64)
+            words = h[:].rearrange("p j t -> p (j t)").bitcast(F32)
             nc.scalar.copy(
                 words.rearrange("p (s j u) -> p s j u", j=P, u=2), turned[:].rearrange("p s u j -> p s j u")
             )
-
-        def quantize(h, j0, width):
             nc.vector.quantize_mx(
                 out=h_codes[:, j0 : j0 + width].bitcast(FP8X4),
                 scales=h_plane[:, j0 : j0 + width],
@@ -154,11 +150,11 @@ def tile_list_gmlpt_sigm_resL_kernel(
             )
 
         def down(j0, width):
+            y = psum_y.tile([P, 2, width], F32, name="y")
             for half in range(2):
                 cols = slice(half * P, (half + 1) * P)
-                y = psum_y.tile([P, width], F32, name="y")
                 nc.tensor.matmul_mx(
-                    out=y[:],
+                    out=y[:, half, :],
                     lhsT=wd_codes[:, cols].bitcast(FP8X4),
                     lhsT_scale=wd_plane[:].bitcast(U8)[:, cols],
                     rhs=h_codes[:, j0 : j0 + width].bitcast(FP8X4),
@@ -166,19 +162,23 @@ def tile_list_gmlpt_sigm_resL_kernel(
                     start=True,
                     stop=True,
                 )
-                y_out = ring.tile([P, width], F32, name="y_out", bufs=4)
-                nc.scalar.copy(y_out[:], y[:])
+            y_out = ring.tile([P, 2, width], F32, name="y_out", bufs=4)
+            nc.scalar.copy(y_out[:], y[:])
+            for half in range(2):
                 result = ring.tile([P, width], F32, name="result", bufs=6)
-                nc.vector.tensor_tensor(result[:], res_table[half][:].indirect(listed(j0, width)), y_out[:], ADD)
-                nc.sync.dma_start(out[cols, j0 : j0 + width], result[:])
+                nc.vector.tensor_tensor(
+                    result[:], res_table[half][:].indirect(listed(j0, width)), y_out[:, half, :], ADD
+                )
+                nc.sync.dma_start(out[half * P : (half + 1) * P, j0 : j0 + width], result[:])
 
-        j0 = 0
-        for width in GROUPS:
-            if j0 % GATHER == 0:
-                gather_last_pass(j0)
-            h = ring.tile([P, width, 4], BF16, name="h", align_bytes=64)
-            for s0 in range(j0, j0 + width, PAIR):
-                turn(h, s0 - j0, [gate(s) for s in range(s0, min(s0 + PAIR, j0 + width), P)])
-            quantize(h, j0, width)
-            down(j0, width)
-            j0 += width
+        starts = [sum(STEPS[:i]) for i in range(len(STEPS))]
+        rows = {}
+        for i in range(len(STEPS) + 2):
+            if i < len(STEPS):
+                if starts[i] % GATHER == 0:
+                    gather_last_pass(starts[i])
+                rows[i] = [gate(s) for s in range(starts[i], starts[i] + STEPS[i], P)]
+            if 1 <= i <= len(STEPS):
+                turn(starts[i - 1], rows[i - 1])
+            if i >= 2:
+                down(starts[i - 2], STEPS[i - 2])

@@ -22,6 +22,7 @@ P = 128
 PASSES = K // 512
 QUADS = 4
 GATHER = 512
+ZERO_SPLIT = 640
 STEPS = [256] * 7 + [128, 128]
 
 
@@ -44,22 +45,23 @@ def tile_list_gmlpt_sigm_resL_kernel(
         w_planes = [keep.tile([P, PASSES, R // 4], I32, name="w_plane%d" % m, align_bytes=64) for m in range(2)]
         wd_plane = keep.tile([P, N // 4], I32, name="wd_plane", align_bytes=64)
         planes = keep.tile([P, PASSES, J // 4], I32, name="planes", align_bytes=64)
-        for tile in (scale_table, wd_plane, planes):
+        nc.vector.memset(w_planes[0][:], 0)
+        nc.gpsimd.memset(w_planes[1][:], 0)
+        nc.vector.memset(scale_table[:, :ZERO_SPLIT], 0)
+        nc.gpsimd.memset(scale_table[:, ZERO_SPLIT:], 0)
+        for tile in (wd_plane, planes):
             nc.vector.memset(tile[:], 0)
-        for tile in w_planes:
-            nc.gpsimd.memset(tile[:], 0)
 
         word_table = [keep.tile([P, T], I32, name="word_table%d" % a, align_bytes=64) for a in range(PASSES)]
         w_codes = [keep.tile([P, PASSES, R // 2], I32, name="w_codes%d" % m, align_bytes=64) for m in range(2)]
-        for m, words in enumerate((wg_words, wu_words)):
-            nc.sync.dma_start(w_codes[m][:], words.bitcast(I32).rearrange("a p n -> p a n"))
+        nc.sync.dma_start(w_codes[0][:], wg_words.bitcast(I32).rearrange("a p n -> p a n"))
         nc.sync.dma_start(scale_table[0:P:4, :], tab_scales.bitcast(I32).rearrange("a q t -> q a t"))
-        for a in range(PASSES):
-            nc.sync.dma_start(word_table[a][:], tab_words[a].rearrange("p t i -> p (t i)").bitcast(I32))
+        nc.sync.dma_start(word_table[0][:], tab_words[0].rearrange("p t i -> p (t i)").bitcast(I32))
+        nc.sync.dma_start(w_codes[1][:], wu_words.bitcast(I32).rearrange("a p n -> p a n"))
+        nc.sync.dma_start(word_table[1][:], tab_words[1].rearrange("p t i -> p (t i)").bitcast(I32))
 
-        for m, scales in enumerate((wg_scales, wu_scales)):
+        for m, (scales, queue) in enumerate(((wg_scales, nc.scalar), (wu_scales, nc.gpsimd))):
             for q in range(QUADS):
-                queue = nc.scalar if m == 0 and q < 3 else nc.gpsimd
                 queue.dma_start(
                     w_planes[m][32 * q : 32 * q + 4, :, :],
                     scales[:, 4 * q : 4 * q + 4, :].bitcast(I32).rearrange("a r n -> r a n"),
@@ -68,22 +70,20 @@ def tile_list_gmlpt_sigm_resL_kernel(
         identity = keep.tile([P, P], F32, name="identity")
         make_identity(nc, identity[:])
 
-        picked_scales = keep.tile([P, J], U8, name="picked_scales", tag="scales_then_residual", align_bytes=64)
+        picked_scales = keep.tile([P, J], U8, name="picked_scales", align_bytes=64)
         nc.vector.tensor_copy(picked_scales[:], scale_table[:].bitcast(U8).indirect(offsets[:]))
         for q in range(QUADS):
             nc.scalar.dma_start(
                 planes[32 * q : 32 * q + 4, :, :], picked_scales[32 * q : 32 * q + 32 : 4, :].bitcast(I32)
             )
 
-        res_table = [
-            keep.tile([P, T], F32, name="res_table0", tag="scales_then_residual", align_bytes=64),
-            keep.tile([P, T], F32, name="res_table1", align_bytes=64),
-        ]
+        res_table = [keep.tile([P, T], F32, name="res_table%d" % half, align_bytes=64) for half in range(2)]
         wd_codes = keep.tile([P, N], I32, name="wd_codes", align_bytes=64)
-        nc.sync.dma_start(res_table[0][:], rT[:P, :])
         nc.sync.dma_start(wd_codes[:], wd_words[0].rearrange("p n i -> p (n i)").bitcast(I32))
         for q in range(QUADS):
             nc.sync.dma_start(wd_plane[32 * q : 32 * q + 4, :], wd_scales[0, 4 * q : 4 * q + 4, :].bitcast(I32))
+            if q == 0:
+                nc.sync.dma_start(res_table[0][:], rT[:P, :])
         nc.sync.dma_start(res_table[1][:], rT[P:, :])
 
         picked_first = keep.tile([P, J], U32, name="picked_first", align_bytes=64)

@@ -23,6 +23,7 @@ PASSES = K // 512
 QUADS = 4
 GATHER = 512
 ZERO_SPLIT = 640
+EARLY_FROM = 1024
 STEPS = [256] * 7 + [128, 128]
 
 
@@ -61,10 +62,9 @@ def tile_list_gmlpt_sigm_resL_kernel(
         nc.sync.dma_start(word_table[1][:], tab_words[1].rearrange("p t i -> p (t i)").bitcast(I32))
 
         for m, (scales, queue) in enumerate(((wg_scales, nc.scalar), (wu_scales, nc.gpsimd))):
-            for q in range(QUADS):
+            for r in range(4):
                 queue.dma_start(
-                    w_planes[m][32 * q : 32 * q + 4, :, :],
-                    scales[:, 4 * q : 4 * q + 4, :].bitcast(I32).rearrange("a r n -> r a n"),
+                    w_planes[m][r:P:32, :, :], scales[:, r:16:4, :].bitcast(I32).rearrange("a q n -> q a n")
                 )
 
         identity = keep.tile([P, P], F32, name="identity")
@@ -72,7 +72,7 @@ def tile_list_gmlpt_sigm_resL_kernel(
 
         picked_scales = keep.tile([P, J], U8, name="picked_scales", align_bytes=64)
         nc.vector.tensor_copy(picked_scales[:], scale_table[:].bitcast(U8).indirect(offsets[:]))
-        for q in range(QUADS):
+        for q in (0, 2, 1, 3):
             nc.scalar.dma_start(
                 planes[32 * q : 32 * q + 4, :, :], picked_scales[32 * q : 32 * q + 32 : 4, :].bitcast(I32)
             )
@@ -80,9 +80,9 @@ def tile_list_gmlpt_sigm_resL_kernel(
         res_table = [keep.tile([P, T], F32, name="res_table%d" % half, align_bytes=64) for half in range(2)]
         wd_codes = keep.tile([P, N], I32, name="wd_codes", align_bytes=64)
         nc.sync.dma_start(wd_codes[:], wd_words[0].rearrange("p n i -> p (n i)").bitcast(I32))
-        for q in range(QUADS):
-            nc.sync.dma_start(wd_plane[32 * q : 32 * q + 4, :], wd_scales[0, 4 * q : 4 * q + 4, :].bitcast(I32))
-            if q == 0:
+        for r in range(4):
+            nc.sync.dma_start(wd_plane[r:P:32, :], wd_scales[0, r:16:4, :].bitcast(I32))
+            if r == 0:
                 nc.sync.dma_start(res_table[0][:], rT[:P, :])
         nc.sync.dma_start(res_table[1][:], rT[P:, :])
 
@@ -101,7 +101,7 @@ def tile_list_gmlpt_sigm_resL_kernel(
         picked_last = {}
 
         def gather_last_pass(j0):
-            picked_last[j0] = ring.tile([P, GATHER], U32, name="picked_last", bufs=2, align_bytes=64)
+            picked_last[j0] = ring.tile([P, GATHER], U32, name="picked_last", bufs=3, align_bytes=64)
             nc.vector.tensor_copy(picked_last[j0][:], word_table[1][:].bitcast(U32).indirect(listed(j0, GATHER)))
 
         def picked(a, j0):
@@ -149,6 +149,8 @@ def tile_list_gmlpt_sigm_resL_kernel(
                 in_=h[:].rearrange("p n t -> p (n t)"),
             )
 
+        early = {}
+
         def down(j0, width):
             y = psum_y.tile([P, 2, width], F32, name="y")
             for half in range(2):
@@ -162,13 +164,21 @@ def tile_list_gmlpt_sigm_resL_kernel(
                     start=True,
                     stop=True,
                 )
+            g0 = j0 - j0 % GATHER
+            fused = range(2) if j0 < EARLY_FROM else range(1, 2)
+            if j0 >= EARLY_FROM and j0 == g0:
+                early[g0] = keep.tile([P, GATHER], F32, name="early%d" % g0)
+                nc.vector.tensor_copy(early[g0][:], res_table[0][:].indirect(listed(g0, GATHER)))
             y_out = ring.tile([P, 2, width], F32, name="y_out", bufs=4)
-            nc.scalar.copy(y_out[:], y[:])
+            nc.scalar.copy(y_out[:, fused.start :, :], y[:, fused.start :, :])
             for half in range(2):
                 result = ring.tile([P, width], F32, name="result", bufs=6)
-                nc.vector.tensor_tensor(
-                    result[:], res_table[half][:].indirect(listed(j0, width)), y_out[:, half, :], ADD
-                )
+                if half in fused:
+                    nc.vector.tensor_tensor(
+                        result[:], res_table[half][:].indirect(listed(j0, width)), y_out[:, half, :], ADD
+                    )
+                else:
+                    nc.vector.tensor_tensor(result[:], y[:, 0, :], early[g0][:, j0 - g0 : j0 - g0 + width], ADD)
                 nc.sync.dma_start(out[half * P : (half + 1) * P, j0 : j0 + width], result[:])
 
         starts = [sum(STEPS[:i]) for i in range(len(STEPS))]

@@ -24,6 +24,7 @@ QUADS = 4
 GATHER = 512
 ZERO_SPLIT = 640
 EARLY_FROM = 1024
+WARM_PASSES = 4
 STEPS = [256] * 7 + [128, 128]
 
 
@@ -93,7 +94,7 @@ def tile_list_gmlpt_sigm_resL_kernel(
         def listed(j0, width):
             return offsets[:, j0 // 16 : (j0 + width) // 16]
 
-        for j0, width in ((0, GATHER), (GATHER, J - GATHER)):
+        for j0, width in ((0, J - GATHER), (J - GATHER, GATHER)):
             nc.vector.tensor_copy(
                 picked_first[:, j0 : j0 + width], word_table[0][:].bitcast(U32).indirect(listed(j0, width))
             )
@@ -180,6 +181,18 @@ def tile_list_gmlpt_sigm_resL_kernel(
                 else:
                     nc.vector.tensor_tensor(result[:], y[:, 0, :], early[g0][:, j0 - g0 : j0 - g0 + width], ADD)
                 nc.sync.dma_start(out[half * P : (half + 1) * P, j0 : j0 + width], result[:])
+
+        warm = psum_y.tile([P, R], F32, name="y")
+        for i in range(WARM_PASSES):
+            nc.tensor.matmul_mx(
+                out=warm[:],
+                lhsT=picked_first[:, 0:P].bitcast(FP8X4),
+                lhsT_scale=picked_scales[:, 0:P],
+                rhs=w_codes[0][:, 0, :].bitcast(FP4X4),
+                rhs_scale=w_planes[0][:, 0, :].bitcast(U8),
+                start=True,
+                stop=True,
+            )
 
         starts = [sum(STEPS[:i]) for i in range(len(STEPS))]
         rows = {}

@@ -22,7 +22,7 @@ P = 128
 PASSES = K // 512
 QUADS = 4
 GATHER = 512
-ZERO_SPLIT = 640
+ZERO_SPLIT = 512
 EARLY_FROM = 1024
 WARM_PASSES = 4
 STEPS = [256] * 7 + [128, 128]
@@ -47,11 +47,10 @@ def tile_list_gmlpt_sigm_resL_kernel(
         w_planes = [keep.tile([P, PASSES, R // 4], I32, name="w_plane%d" % m, align_bytes=64) for m in range(2)]
         wd_plane = keep.tile([P, N // 4], I32, name="wd_plane", align_bytes=64)
         planes = keep.tile([P, PASSES, J // 4], I32, name="planes", align_bytes=64)
-        nc.vector.memset(w_planes[0][:], 0)
-        nc.gpsimd.memset(w_planes[1][:], 0)
+        nc.gpsimd.memset(w_planes[0][:], 0)
         nc.vector.memset(scale_table[:, :ZERO_SPLIT], 0)
         nc.gpsimd.memset(scale_table[:, ZERO_SPLIT:], 0)
-        for tile in (wd_plane, planes):
+        for tile in (w_planes[1], wd_plane, planes):
             nc.vector.memset(tile[:], 0)
 
         word_table = [keep.tile([P, T], I32, name="word_table%d" % a, align_bytes=64) for a in range(PASSES)]
@@ -128,9 +127,10 @@ def tile_list_gmlpt_sigm_resL_kernel(
             ga = project(psum_gate, 0, j0)
             ub = project(psum_up, 1, j0)
             sig = ring.tile([P, 2, P, 2], F32, name="sig")
-            nc.scalar.activation(sig[:], ga, SIGMOID)
             h_rows = ring.tile([P, 2, P, 2], BF16, name="h_rows", bufs=6)
-            nc.vector.tensor_tensor(h_rows[:], ub, sig[:], MULT)
+            nc.scalar.activation(sig[:], ga, SIGMOID)
+            for part in [slice(0, 1), slice(1, 2)] if j0 == J - P else [slice(0, 2)]:
+                nc.vector.tensor_tensor(h_rows[:, part], ub[:, part], sig[:, part], MULT)
             return h_rows[:].rearrange("j u p e -> j (u p e)").bitcast(F32)
 
         def turn(j0, rows):
@@ -168,7 +168,7 @@ def tile_list_gmlpt_sigm_resL_kernel(
             g0 = j0 - j0 % GATHER
             fused = range(2) if j0 < EARLY_FROM else range(1, 2)
             if j0 >= EARLY_FROM and j0 == g0:
-                early[g0] = keep.tile([P, GATHER], F32, name="early%d" % g0)
+                early[g0] = ring.tile([P, GATHER], F32, name="early", tag="picked_last" if g0 > EARLY_FROM else "early", bufs=3 if g0 > EARLY_FROM else 1, align_bytes=64)
                 nc.vector.tensor_copy(early[g0][:], res_table[0][:].indirect(listed(g0, GATHER)))
             y_out = ring.tile([P, 2, width], F32, name="y_out", bufs=4)
             nc.scalar.copy(y_out[:, fused.start :, :], y[:, fused.start :, :])

@@ -58,8 +58,8 @@ def tile_list_gmlpt_sigm_resL_kernel(
         nc.sync.dma_start(w_codes[0][:], wg_words.bitcast(I32).rearrange("a p n -> p a n"))
         nc.sync.dma_start(scale_table[0:P:4, :], tab_scales.bitcast(I32).rearrange("a q t -> q a t"))
         nc.sync.dma_start(word_table[0][:], tab_words[0].rearrange("p t i -> p (t i)").bitcast(I32))
-        nc.sync.dma_start(w_codes[1][:], wu_words.bitcast(I32).rearrange("a p n -> p a n"))
         nc.sync.dma_start(word_table[1][:], tab_words[1].rearrange("p t i -> p (t i)").bitcast(I32))
+        nc.sync.dma_start(w_codes[1][:], wu_words.bitcast(I32).rearrange("a p n -> p a n"))
 
         for m, (scales, queue) in enumerate(((wg_scales, nc.scalar), (wu_scales, nc.gpsimd))):
             for r in range(4):

@@ -22,9 +22,9 @@ P = 128
 PASSES = K // 512
 QUADS = 4
 GATHER = 512
-ZERO_SPLIT = 512
+FIRST_PLANES = 1024
 EARLY_FROM = 1024
-WARM_PASSES = 4
+WARM_PASSES = 3
 STEPS = [256] * 7 + [128, 128]
 
 
@@ -46,17 +46,21 @@ def tile_list_gmlpt_sigm_resL_kernel(
         scale_table = keep.tile([P, T // 4], I32, name="scale_table", align_bytes=64)
         w_planes = [keep.tile([P, PASSES, R // 4], I32, name="w_plane%d" % m, align_bytes=64) for m in range(2)]
         wd_plane = keep.tile([P, N // 4], I32, name="wd_plane", align_bytes=64)
-        planes = keep.tile([P, PASSES, J // 4], I32, name="planes", align_bytes=64)
+        spans = ((0, FIRST_PLANES), (FIRST_PLANES, J))
+        planes = [keep.tile([P, PASSES, (b - a) // 4], I32, name="planes%d" % a, align_bytes=64) for a, b in spans]
         nc.gpsimd.memset(w_planes[0][:], 0)
-        nc.vector.memset(scale_table[:, :ZERO_SPLIT], 0)
-        nc.gpsimd.memset(scale_table[:, ZERO_SPLIT:], 0)
-        for tile in (w_planes[1], wd_plane, planes):
+        nc.vector.memset(scale_table[64:, :], 0)
+        nc.gpsimd.memset(scale_table[32:64, :], 0)
+        for tile in (w_planes[1], wd_plane, *planes):
             nc.vector.memset(tile[:], 0)
+
+        table_in = keep.tile([P, 1], F32, name="table_in")
+        nc.vector.memset(table_in[:], 0.0)
 
         word_table = [keep.tile([P, T], I32, name="word_table%d" % a, align_bytes=64) for a in range(PASSES)]
         w_codes = [keep.tile([P, PASSES, R // 2], I32, name="w_codes%d" % m, align_bytes=64) for m in range(2)]
+        nc.sync.dma_start(scale_table[:32, :], tab_scales.bitcast(I32).rearrange("a q t -> q a t"))
         nc.sync.dma_start(w_codes[0][:], wg_words.bitcast(I32).rearrange("a p n -> p a n"))
-        nc.sync.dma_start(scale_table[0:P:4, :], tab_scales.bitcast(I32).rearrange("a q t -> q a t"))
         nc.sync.dma_start(word_table[0][:], tab_words[0].rearrange("p t i -> p (t i)").bitcast(I32))
         nc.sync.dma_start(word_table[1][:], tab_words[1].rearrange("p t i -> p (t i)").bitcast(I32))
         nc.sync.dma_start(w_codes[1][:], wu_words.bitcast(I32).rearrange("a p n -> p a n"))
@@ -70,20 +74,26 @@ def tile_list_gmlpt_sigm_resL_kernel(
         identity = keep.tile([P, P], F32, name="identity")
         make_identity(nc, identity[:])
 
-        picked_scales = keep.tile([P, J], U8, name="picked_scales", align_bytes=64)
-        nc.vector.tensor_copy(picked_scales[:], scale_table[:].bitcast(U8).indirect(offsets[:]))
-        for q in (0, 2, 1, 3):
-            nc.scalar.dma_start(
-                planes[32 * q : 32 * q + 4, :, :], picked_scales[32 * q : 32 * q + 32 : 4, :].bitcast(I32)
-            )
+        picked_scales = [keep.tile([P, b - a], U8, name="picked_scales%d" % a, align_bytes=64) for a, b in spans]
+        for picked_part, (a, b) in zip(picked_scales, spans):
+            nc.vector.tensor_copy(picked_part[:], scale_table[:].bitcast(U8).indirect(offsets[:, a // 16 : b // 16]))
+
+        def lay_planes(part):
+            for q in (0, 2, 1, 3):
+                nc.scalar.dma_start(
+                    planes[part][32 * q : 32 * q + 4, :, :], picked_scales[part][8 * q : 8 * q + 8, :].bitcast(I32)
+                )
+
+        lay_planes(0)
+        table_out = keep.tile([P, 1], F32, name="table_out", tag="scale_table", align_bytes=64)
+        nc.scalar.activation(table_out[:], table_in[:], SIGMOID)
 
         res_table = [keep.tile([P, T], F32, name="res_table%d" % half, align_bytes=64) for half in range(2)]
         wd_codes = keep.tile([P, N], I32, name="wd_codes", align_bytes=64)
+        nc.sync.dma_start(res_table[0][:], rT[:P, :])
         nc.sync.dma_start(wd_codes[:], wd_words[0].rearrange("p n i -> p (n i)").bitcast(I32))
         for r in range(4):
             nc.sync.dma_start(wd_plane[r:P:32, :], wd_scales[0, r:16:4, :].bitcast(I32))
-            if r == 0:
-                nc.sync.dma_start(res_table[0][:], rT[:P, :])
         nc.sync.dma_start(res_table[1][:], rT[P:, :])
 
         picked_first = keep.tile([P, J], U32, name="picked_first", align_bytes=64)
@@ -109,13 +119,18 @@ def tile_list_gmlpt_sigm_resL_kernel(
                 return picked_first[:, j0 : j0 + P]
             return picked_last[j0 - j0 % GATHER][:, j0 % GATHER : j0 % GATHER + P]
 
+        def plane_of(a, j0):
+            late = j0 >= FIRST_PLANES
+            at = j0 - late * FIRST_PLANES
+            return planes[late][:, a, :].bitcast(U8)[:, at : at + P]
+
         def project(pool, m, j0):
             acc = pool.tile([P, R], F32, name="acc%d" % m)
             for a in range(PASSES):
                 nc.tensor.matmul_mx(
                     out=acc[:],
                     lhsT=picked(a, j0).bitcast(FP8X4),
-                    lhsT_scale=planes[:, a, :].bitcast(U8)[:, j0 : j0 + P],
+                    lhsT_scale=plane_of(a, j0),
                     rhs=w_codes[m][:, a, :].bitcast(FP4X4),
                     rhs_scale=w_planes[m][:, a, :].bitcast(U8),
                     start=(a == 0),
@@ -187,12 +202,14 @@ def tile_list_gmlpt_sigm_resL_kernel(
             nc.tensor.matmul_mx(
                 out=warm[:],
                 lhsT=picked_first[:, 0:P].bitcast(FP8X4),
-                lhsT_scale=picked_scales[:, 0:P],
+                lhsT_scale=plane_of(0, FIRST_PLANES),
                 rhs=w_codes[0][:, 0, :].bitcast(FP4X4),
                 rhs_scale=w_planes[0][:, 0, :].bitcast(U8),
                 start=True,
                 stop=True,
             )
+
+        lay_planes(1)
 
         starts = [sum(STEPS[:i]) for i in range(len(STEPS))]
         rows = {}

@@ -24,7 +24,7 @@ QUADS = 4
 GATHER = 512
 FIRST_PLANES = 1024
 EARLY_FROM = 1024
-WARM_PASSES = 3
+WARM_PASSES = 5
 STEPS = [256] * 7 + [128, 128]
 
 
@@ -49,21 +49,18 @@ def tile_list_gmlpt_sigm_resL_kernel(
         spans = ((0, FIRST_PLANES), (FIRST_PLANES, J))
         planes = [keep.tile([P, PASSES, (b - a) // 4], I32, name="planes%d" % a, align_bytes=64) for a, b in spans]
         nc.gpsimd.memset(w_planes[0][:], 0)
+        nc.vector.memset(w_planes[1][:], 0)
         nc.vector.memset(scale_table[64:, :], 0)
-        nc.gpsimd.memset(scale_table[32:64, :], 0)
-        for tile in (w_planes[1], wd_plane, *planes):
+        nc.vector.memset(scale_table[32:64, :], 0)
+        for tile in (wd_plane, *planes):
             nc.vector.memset(tile[:], 0)
-
-        table_in = keep.tile([P, 1], F32, name="table_in")
-        nc.vector.memset(table_in[:], 0.0)
 
         word_table = [keep.tile([P, T], I32, name="word_table%d" % a, align_bytes=64) for a in range(PASSES)]
         w_codes = [keep.tile([P, PASSES, R // 2], I32, name="w_codes%d" % m, align_bytes=64) for m in range(2)]
         nc.sync.dma_start(scale_table[:32, :], tab_scales.bitcast(I32).rearrange("a q t -> q a t"))
-        nc.sync.dma_start(w_codes[0][:], wg_words.bitcast(I32).rearrange("a p n -> p a n"))
         nc.sync.dma_start(word_table[0][:], tab_words[0].rearrange("p t i -> p (t i)").bitcast(I32))
+        nc.sync.dma_start(w_codes[0][:, 0, :], wg_words[0].bitcast(I32))
         nc.sync.dma_start(word_table[1][:], tab_words[1].rearrange("p t i -> p (t i)").bitcast(I32))
-        nc.sync.dma_start(w_codes[1][:], wu_words.bitcast(I32).rearrange("a p n -> p a n"))
 
         for m, (scales, queue) in enumerate(((wg_scales, nc.scalar), (wu_scales, nc.gpsimd))):
             for r in range(4):
@@ -80,13 +77,13 @@ def tile_list_gmlpt_sigm_resL_kernel(
 
         def lay_planes(part):
             for q in (0, 2, 1, 3):
-                nc.scalar.dma_start(
+                (nc.sync, nc.gpsimd)[part].dma_start(
                     planes[part][32 * q : 32 * q + 4, :, :], picked_scales[part][8 * q : 8 * q + 8, :].bitcast(I32)
                 )
 
         lay_planes(0)
-        table_out = keep.tile([P, 1], F32, name="table_out", tag="scale_table", align_bytes=64)
-        nc.scalar.activation(table_out[:], table_in[:], SIGMOID)
+        nc.sync.dma_start(w_codes[0][:, 1, :], wg_words[1].bitcast(I32))
+        nc.sync.dma_start(w_codes[1][:], wu_words.bitcast(I32).rearrange("a p n -> p a n"))
 
         res_table = [keep.tile([P, T], F32, name="res_table%d" % half, align_bytes=64) for half in range(2)]
         wd_codes = keep.tile([P, N], I32, name="wd_codes", align_bytes=64)
@@ -103,7 +100,7 @@ def tile_list_gmlpt_sigm_resL_kernel(
         def listed(j0, width):
             return offsets[:, j0 // 16 : (j0 + width) // 16]
 
-        for j0, width in ((0, J - GATHER), (J - GATHER, GATHER)):
+        for j0, width in ((0, 1024), (1024, J - 1024)):
             nc.vector.tensor_copy(
                 picked_first[:, j0 : j0 + width], word_table[0][:].bitcast(U32).indirect(listed(j0, width))
             )

@@ -50,14 +50,16 @@ def tile_list_gmlpt_sigm_resL_kernel(
         planes = [keep.tile([P, PASSES, (b - a) // 4], I32, name="planes%d" % a, align_bytes=64) for a, b in spans]
         nc.gpsimd.memset(w_planes[0][:], 0)
         nc.vector.memset(w_planes[1][:], 0)
-        nc.vector.memset(scale_table[64:, :], 0)
-        nc.vector.memset(scale_table[32:64, :], 0)
+        nc.vector.memset(scale_table[:96, :], 0)
         for tile in (wd_plane, *planes):
             nc.vector.memset(tile[:], 0)
 
+        zeros = keep.tile([P, P], F32, name="zeros")
+        nc.vector.memset(zeros[:], 0.0)
+
         word_table = [keep.tile([P, T], I32, name="word_table%d" % a, align_bytes=64) for a in range(PASSES)]
         w_codes = [keep.tile([P, PASSES, R // 2], I32, name="w_codes%d" % m, align_bytes=64) for m in range(2)]
-        nc.sync.dma_start(scale_table[:32, :], tab_scales.bitcast(I32).rearrange("a q t -> q a t"))
+        nc.sync.dma_start(scale_table[96:, :], tab_scales.bitcast(I32).rearrange("a q t -> q a t"))
         nc.sync.dma_start(word_table[0][:], tab_words[0].rearrange("p t i -> p (t i)").bitcast(I32))
         nc.sync.dma_start(w_codes[0][:, 0, :], wg_words[0].bitcast(I32))
         nc.sync.dma_start(word_table[1][:], tab_words[1].rearrange("p t i -> p (t i)").bitcast(I32))
@@ -71,14 +73,13 @@ def tile_list_gmlpt_sigm_resL_kernel(
         identity = keep.tile([P, P], F32, name="identity")
         make_identity(nc, identity[:])
 
-        picked_scales = [keep.tile([P, b - a], U8, name="picked_scales%d" % a, align_bytes=64) for a, b in spans]
-        for picked_part, (a, b) in zip(picked_scales, spans):
-            nc.vector.tensor_copy(picked_part[:], scale_table[:].bitcast(U8).indirect(offsets[:, a // 16 : b // 16]))
+        picked_scales = keep.tile([P, J], U8, name="picked_scales", align_bytes=64)
+        nc.vector.tensor_copy(picked_scales[:], scale_table[:].bitcast(U8).indirect(offsets[:]))
 
         def lay_planes(part):
             for q in (0, 2, 1, 3):
                 (nc.sync, nc.gpsimd)[part].dma_start(
-                    planes[part][32 * q : 32 * q + 4, :, :], picked_scales[part][8 * q : 8 * q + 8, :].bitcast(I32)
+                    planes[part][32 * q : 32 * q + 4, :, :], picked_scales[96 + 8 * q : 104 + 8 * q, spans[part][0] : spans[part][1]].bitcast(I32)
                 )
 
         lay_planes(0)
@@ -151,7 +152,10 @@ def tile_list_gmlpt_sigm_resL_kernel(
                 for u in range(2):
                     nc.tensor.transpose(turned[:, s, u, :], rows[s][:, u * P : (u + 1) * P], identity[:])
             width = len(rows) * P
-            h = ring.tile([P, width, 4], BF16, name="h", align_bytes=64)
+            if j0 == J - P:
+                h = keep.tile([P, width, 4], BF16, name="h", tag="h_last", align_bytes=64)
+            else:
+                h = ring.tile([P, width, 4], BF16, name="h", align_bytes=64)
             words = h[:].rearrange("p j t -> p (j t)").bitcast(F32)
             nc.scalar.copy(
                 words.rearrange("p (s j u) -> p s j u", j=P, u=2), turned[:].rearrange("p s u j -> p s j u")
@@ -182,6 +186,14 @@ def tile_list_gmlpt_sigm_resL_kernel(
             if j0 >= EARLY_FROM and j0 == g0:
                 early[g0] = ring.tile([P, GATHER], F32, name="early", tag="picked_last" if g0 > EARLY_FROM else "early", bufs=3 if g0 > EARLY_FROM else 1, align_bytes=64)
                 nc.vector.tensor_copy(early[g0][:], res_table[0][:].indirect(listed(g0, GATHER)))
+            if j0 == J - P:
+                last = keep.tile([P, P], F32, name="last", tag="h_last", align_bytes=64)
+                nc.vector.tensor_tensor(last[:], res_table[1][:].indirect(listed(j0, width)), zeros[:], ADD)
+                result = keep.tile([P, 2, P], F32, name="last_result")
+                nc.vector.tensor_tensor(result[:, 0, :], y[:, 0, :], early[g0][:, j0 - g0 :], ADD)
+                nc.vector.tensor_tensor(result[:, 1, :], y[:, 1, :], last[:], ADD)
+                nc.sync.dma_start(out.rearrange("(h p) j -> p h j", h=2)[:, :, j0:], result[:])
+                return
             y_out = ring.tile([P, 2, width], F32, name="y_out", bufs=4)
             nc.scalar.copy(y_out[:, fused.start :, :], y[:, fused.start :, :])
             for half in range(2):

@@ -23,7 +23,16 @@ PASSES = K // 512
 QUADS = 4
 GATHER = 512
 FIRST_PLANES = 1024
-EARLY_FROM = 1024
+POOL = [4, 5, 6, 7, 8, 9]
+PACE = {2: (0, 0), 3: (0, 1), 4: (0, 2), 5: (0, 3), 6: (1, 0), 7: (1, 1), 8: (1, 2), 9: (1, 3)}
+LOADS = ["wg1", "wu", "res0", "wd", "res1"]
+LATE_QUEUE = "gpsimd"
+BANKS = (2, 3, 1, 2)
+LAST_BUFS = 3
+LAG_TURN, LAG_DOWN, LAG_ADD = 1, 2, 3
+POOL_SPLIT = 1
+WDS_POOL = False
+PRE_WD = False
 WARM_PASSES = 5
 STEPS = [256] * 7 + [128, 128]
 
@@ -35,10 +44,10 @@ def tile_list_gmlpt_sigm_resL_kernel(
     with ExitStack() as ctx:
         keep = ctx.enter_context(tc.tile_pool(name="keep", bufs=1))
         ring = ctx.enter_context(tc.tile_pool(name="ring", bufs=3))
-        psum_gate = ctx.enter_context(tc.psum_pool(name="psum_gate", bufs=2))
-        psum_up = ctx.enter_context(tc.psum_pool(name="psum_up", bufs=3))
-        psum_turn = ctx.enter_context(tc.psum_pool(name="psum_turn", bufs=1))
-        psum_y = ctx.enter_context(tc.psum_pool(name="psum_y", bufs=2))
+        psum_gate = ctx.enter_context(tc.psum_pool(name="psum_gate", bufs=BANKS[0]))
+        psum_up = ctx.enter_context(tc.psum_pool(name="psum_up", bufs=BANKS[1]))
+        psum_turn = ctx.enter_context(tc.psum_pool(name="psum_turn", bufs=BANKS[2]))
+        psum_y = ctx.enter_context(tc.psum_pool(name="psum_y", bufs=BANKS[3]))
 
         offsets = keep.tile([P, J // 16], U16, name="offsets")
         nc.sync.dma_start(offsets[:], offs)
@@ -54,14 +63,15 @@ def tile_list_gmlpt_sigm_resL_kernel(
         for tile in (wd_plane, *planes):
             nc.vector.memset(tile[:], 0)
 
-        zeros = keep.tile([P, P], F32, name="zeros")
-        nc.vector.memset(zeros[:], 0.0)
-
         word_table = [keep.tile([P, T], I32, name="word_table%d" % a, align_bytes=64) for a in range(PASSES)]
         w_codes = [keep.tile([P, PASSES, R // 2], I32, name="w_codes%d" % m, align_bytes=64) for m in range(2)]
         nc.sync.dma_start(scale_table[96:, :], tab_scales.bitcast(I32).rearrange("a q t -> q a t"))
         nc.sync.dma_start(word_table[0][:], tab_words[0].rearrange("p t i -> p (t i)").bitcast(I32))
-        nc.sync.dma_start(w_codes[0][:, 0, :], wg_words[0].bitcast(I32))
+        wd_codes = keep.tile([P, N], I32, name="wd_codes", align_bytes=64)
+        if PRE_WD:
+            nc.sync.dma_start(wd_codes[:], wd_words[0].rearrange("p n i -> p (n i)").bitcast(I32))
+        else:
+            nc.sync.dma_start(w_codes[0][:, 0, :], wg_words[0].bitcast(I32))
         nc.sync.dma_start(word_table[1][:], tab_words[1].rearrange("p t i -> p (t i)").bitcast(I32))
 
         for m, (scales, queue) in enumerate(((wg_scales, nc.scalar), (wu_scales, nc.gpsimd))):
@@ -69,6 +79,10 @@ def tile_list_gmlpt_sigm_resL_kernel(
                 queue.dma_start(
                     w_planes[m][r:P:32, :, :], scales[:, r:16:4, :].bitcast(I32).rearrange("a q n -> q a n")
                 )
+
+        if WDS_POOL:
+            for r in range(4):
+                nc.gpsimd.dma_start(wd_plane[r:P:32, :], wd_scales[0, r:16:4, :].bitcast(I32))
 
         identity = keep.tile([P, P], F32, name="identity")
         make_identity(nc, identity[:])
@@ -78,21 +92,30 @@ def tile_list_gmlpt_sigm_resL_kernel(
 
         def lay_planes(part):
             for q in (0, 2, 1, 3):
-                (nc.sync, nc.gpsimd)[part].dma_start(
+                (nc.sync, {"gpsimd": nc.gpsimd, "sync": nc.sync, "scalar": nc.scalar}[LATE_QUEUE])[part].dma_start(
                     planes[part][32 * q : 32 * q + 4, :, :], picked_scales[96 + 8 * q : 104 + 8 * q, spans[part][0] : spans[part][1]].bitcast(I32)
                 )
 
         lay_planes(0)
-        nc.sync.dma_start(w_codes[0][:, 1, :], wg_words[1].bitcast(I32))
-        nc.sync.dma_start(w_codes[1][:], wu_words.bitcast(I32).rearrange("a p n -> p a n"))
-
         res_table = [keep.tile([P, T], F32, name="res_table%d" % half, align_bytes=64) for half in range(2)]
-        wd_codes = keep.tile([P, N], I32, name="wd_codes", align_bytes=64)
-        nc.sync.dma_start(res_table[0][:], rT[:P, :])
-        nc.sync.dma_start(wd_codes[:], wd_words[0].rearrange("p n i -> p (n i)").bitcast(I32))
-        for r in range(4):
-            nc.sync.dma_start(wd_plane[r:P:32, :], wd_scales[0, r:16:4, :].bitcast(I32))
-        nc.sync.dma_start(res_table[1][:], rT[P:, :])
+        for what in LOADS:
+            if what == "wg1":
+                nc.sync.dma_start(w_codes[0][:, 1, :], wg_words[1].bitcast(I32))
+            if what == "wg":
+                nc.sync.dma_start(w_codes[0][:], wg_words.bitcast(I32).rearrange("a p n -> p a n"))
+            if what == "wu":
+                nc.sync.dma_start(w_codes[1][:], wu_words.bitcast(I32).rearrange("a p n -> p a n"))
+            if what in ("wu0", "wu1"):
+                nc.sync.dma_start(w_codes[1][:, int(what[2]), :], wu_words[int(what[2])].bitcast(I32))
+            if what in ("res0", "res1"):
+                nc.sync.dma_start(res_table[int(what[3])][:], rT[int(what[3]) * P : int(what[3]) * P + P, :])
+            if what in ("wd", "wdw"):
+                nc.sync.dma_start(wd_codes[:], wd_words[0].rearrange("p n i -> p (n i)").bitcast(I32))
+            if what in ("wd", "wds"):
+                for r in range(4):
+                    nc.sync.dma_start(wd_plane[r:P:32, :], wd_scales[0, r:16:4, :].bitcast(I32))
+            if what == "late":
+                lay_planes(1)
 
         picked_first = keep.tile([P, J], U32, name="picked_first", align_bytes=64)
         h_codes = keep.tile([P, J], U32, name="h_codes", align_bytes=64)
@@ -109,7 +132,7 @@ def tile_list_gmlpt_sigm_resL_kernel(
         picked_last = {}
 
         def gather_last_pass(j0):
-            picked_last[j0] = ring.tile([P, GATHER], U32, name="picked_last", bufs=3, align_bytes=64)
+            picked_last[j0] = ring.tile([P, GATHER], U32, name="picked_last", bufs=LAST_BUFS, align_bytes=64)
             nc.vector.tensor_copy(picked_last[j0][:], word_table[1][:].bitcast(U32).indirect(listed(j0, GATHER)))
 
         def picked(a, j0):
@@ -136,14 +159,32 @@ def tile_list_gmlpt_sigm_resL_kernel(
                 )
             return acc[:].rearrange("j (p u e) -> j u p e", u=2, e=2)
 
+        residual = [keep.tile([P, 2, GATHER], F32, name="residual%d" % g, align_bytes=64) for g in range(J // GATHER)]
+
         def gate(j0):
             ga = project(psum_gate, 0, j0)
             ub = project(psum_up, 1, j0)
-            sig = ring.tile([P, 2, P, 2], F32, name="sig")
+            tile = j0 // P
+            if tile in PACE:
+                half, group = PACE[tile]
+                sig = residual[group][:, half, :]
+            else:
+                sig = ring.tile([P, R], F32, name="sig")[:]
             h_rows = ring.tile([P, 2, P, 2], BF16, name="h_rows", bufs=6)
-            nc.scalar.activation(sig[:], ga, SIGMOID)
-            for part in [slice(0, 1), slice(1, 2)] if j0 == J - P else [slice(0, 2)]:
-                nc.vector.tensor_tensor(h_rows[:, part], ub[:, part], sig[:, part], MULT)
+            sig4 = sig.rearrange("j (u p e) -> j u p e", u=2, e=2)
+            nc.scalar.activation(sig4, ga, SIGMOID)
+            if tile in POOL:
+                up = ring.tile([P, 2, P, 2], F32, name="up")
+                nc.scalar.copy(up[:], ub)
+                flat = [x.rearrange("j u p e -> j (u p e)") for x in (h_rows[:], up[:])]
+                for k in range(POOL_SPLIT):
+                    part = slice(k * R // POOL_SPLIT, (k + 1) * R // POOL_SPLIT)
+                    nc.gpsimd.tensor_tensor(flat[0][:, part], flat[1][:, part], sig[:, part], MULT)
+            else:
+                for part in [slice(0, 1), slice(1, 2)] if j0 == J - P else [slice(0, 2)]:
+                    nc.vector.tensor_tensor(h_rows[:, part], ub[:, part], sig4[:, part], MULT)
+            if tile in PACE:
+                nc.vector.tensor_copy(sig, res_table[half][:].indirect(listed(group * GATHER, GATHER)))
             return h_rows[:].rearrange("j u p e -> j (u p e)").bitcast(F32)
 
         def turn(j0, rows):
@@ -152,10 +193,7 @@ def tile_list_gmlpt_sigm_resL_kernel(
                 for u in range(2):
                     nc.tensor.transpose(turned[:, s, u, :], rows[s][:, u * P : (u + 1) * P], identity[:])
             width = len(rows) * P
-            if j0 == J - P:
-                h = keep.tile([P, width, 4], BF16, name="h", tag="h_last", align_bytes=64)
-            else:
-                h = ring.tile([P, width, 4], BF16, name="h", align_bytes=64)
+            h = ring.tile([P, width, 4], BF16, name="h", align_bytes=64)
             words = h[:].rearrange("p j t -> p (j t)").bitcast(F32)
             nc.scalar.copy(
                 words.rearrange("p (s j u) -> p s j u", j=P, u=2), turned[:].rearrange("p s u j -> p s j u")
@@ -166,7 +204,8 @@ def tile_list_gmlpt_sigm_resL_kernel(
                 in_=h[:].rearrange("p n t -> p (n t)"),
             )
 
-        early = {}
+        sums = {}
+        outs = {}
 
         def down(j0, width):
             y = psum_y.tile([P, 2, width], F32, name="y")
@@ -181,53 +220,60 @@ def tile_list_gmlpt_sigm_resL_kernel(
                     start=True,
                     stop=True,
                 )
-            g0 = j0 - j0 % GATHER
-            fused = range(2) if j0 < EARLY_FROM else range(1, 2)
-            if j0 >= EARLY_FROM and j0 == g0:
-                early[g0] = ring.tile([P, GATHER], F32, name="early", tag="picked_last" if g0 > EARLY_FROM else "early", bufs=3 if g0 > EARLY_FROM else 1, align_bytes=64)
-                nc.vector.tensor_copy(early[g0][:], res_table[0][:].indirect(listed(g0, GATHER)))
-            if j0 == J - P:
-                last = keep.tile([P, P], F32, name="last", tag="h_last", align_bytes=64)
-                nc.vector.tensor_tensor(last[:], res_table[1][:].indirect(listed(j0, width)), zeros[:], ADD)
-                result = keep.tile([P, 2, P], F32, name="last_result")
-                nc.vector.tensor_tensor(result[:, 0, :], y[:, 0, :], early[g0][:, j0 - g0 :], ADD)
-                nc.vector.tensor_tensor(result[:, 1, :], y[:, 1, :], last[:], ADD)
-                nc.sync.dma_start(out.rearrange("(h p) j -> p h j", h=2)[:, :, j0:], result[:])
+            sums[j0] = y
+            fused = [h for h in range(2) if (h, j0 // GATHER) not in [PACE[t] for t in PACE]]
+            if fused:
+                y_out = ring.tile([P, 2, width], F32, name="y_out", bufs=6)
+                nc.scalar.copy(y_out[:, fused[0] : fused[-1] + 1, :], y[:, fused[0] : fused[-1] + 1, :])
+                outs[j0] = y_out
+
+        def finish(j0, width):
+            fused = [h for h in range(2) if (h, j0 // GATHER) not in [PACE[t] for t in PACE]]
+            picked_res = residual[j0 // GATHER][:, :, j0 % GATHER : j0 % GATHER + width]
+            if not fused:
+                result = ring.tile([P, 2, width], F32, name="result", bufs=6)
+                nc.vector.tensor_tensor(result[:], sums[j0][:], picked_res, ADD)
+                nc.sync.dma_start(out.rearrange("(h p) j -> p h j", h=2)[:, :, j0 : j0 + width], result[:])
                 return
-            y_out = ring.tile([P, 2, width], F32, name="y_out", bufs=4)
-            nc.scalar.copy(y_out[:, fused.start :, :], y[:, fused.start :, :])
             for half in range(2):
                 result = ring.tile([P, width], F32, name="result", bufs=6)
                 if half in fused:
                     nc.vector.tensor_tensor(
-                        result[:], res_table[half][:].indirect(listed(j0, width)), y_out[:, half, :], ADD
+                        result[:], res_table[half][:].indirect(listed(j0, width)), outs[j0][:, half, :], ADD
                     )
                 else:
-                    nc.vector.tensor_tensor(result[:], y[:, 0, :], early[g0][:, j0 - g0 : j0 - g0 + width], ADD)
+                    nc.vector.tensor_tensor(result[:], sums[j0][:, half, :], picked_res[:, half, :], ADD)
                 nc.sync.dma_start(out[half * P : (half + 1) * P, j0 : j0 + width], result[:])
 
         warm = psum_y.tile([P, R], F32, name="y")
         for i in range(WARM_PASSES):
             nc.tensor.matmul_mx(
-                out=warm[:],
+                out=warm[:, :N] if PRE_WD else warm[:],
                 lhsT=picked_first[:, 0:P].bitcast(FP8X4),
                 lhsT_scale=plane_of(0, FIRST_PLANES),
-                rhs=w_codes[0][:, 0, :].bitcast(FP4X4),
-                rhs_scale=w_planes[0][:, 0, :].bitcast(U8),
+                rhs=wd_codes[:].bitcast(FP8X4) if PRE_WD else w_codes[0][:, 0, :].bitcast(FP4X4),
+                rhs_scale=planes[1][:, 1, :N // 4].bitcast(U8) if PRE_WD else w_planes[0][:, 0, :].bitcast(U8),
                 start=True,
                 stop=True,
             )
 
-        lay_planes(1)
+        if "late" not in LOADS:
+            lay_planes(1)
 
         starts = [sum(STEPS[:i]) for i in range(len(STEPS))]
         rows = {}
-        for i in range(len(STEPS) + 2):
+        for i in range(len(STEPS) + LAG_ADD):
             if i < len(STEPS):
-                if starts[i] % GATHER == 0:
-                    gather_last_pass(starts[i])
-                rows[i] = [gate(s) for s in range(starts[i], starts[i] + STEPS[i], P)]
-            if 1 <= i <= len(STEPS):
-                turn(starts[i - 1], rows[i - 1])
-            if i >= 2:
-                down(starts[i - 2], STEPS[i - 2])
+                for s in range(starts[i], starts[i] + STEPS[i], P):
+                    if s % GATHER == 0:
+                        gather_last_pass(s)
+                    rows[s] = gate(s)
+            if 0 <= i - LAG_TURN < len(STEPS):
+                at = starts[i - LAG_TURN]
+                turn(at, [rows[s] for s in range(at, at + STEPS[i - LAG_TURN], P)])
+            if LAG_ADD > LAG_DOWN and 0 <= i - LAG_ADD < len(STEPS):
+                finish(starts[i - LAG_ADD], STEPS[i - LAG_ADD])
+            if 0 <= i - LAG_DOWN < len(STEPS):
+                down(starts[i - LAG_DOWN], STEPS[i - LAG_DOWN])
+            if LAG_ADD == LAG_DOWN and 0 <= i - LAG_ADD < len(STEPS):
+                finish(starts[i - LAG_ADD], STEPS[i - LAG_ADD])

@@ -23,17 +23,25 @@ PASSES = K // 512
 QUADS = 4
 GATHER = 512
 FIRST_PLANES = 1024
-POOL = [4, 5, 6, 7, 8, 9]
+POOL = [2, 3, 4, 5, 6, 7, 8, 9, 10, 11, 12]
 PACE = {2: (0, 0), 3: (0, 1), 4: (0, 2), 5: (0, 3), 6: (1, 0), 7: (1, 1), 8: (1, 2), 9: (1, 3)}
-LOADS = ["wg1", "wu", "res0", "wd", "res1"]
+LOADS = ["wu", "wg1", "res0", "wdw", "res1", "wds"]
 LATE_QUEUE = "gpsimd"
 BANKS = (2, 3, 1, 2)
 LAST_BUFS = 3
-LAG_TURN, LAG_DOWN, LAG_ADD = 1, 2, 3
+LAG_TURN = 2
+LAG_DOWN = 6
+LAG_ADD = 8
+PAIRED_UPTO = 8
+HOLD_FROM = 16
+BORROW_T = 2
+BORROW_Y = 3
+TAIL = "stages"
+H_ROWS = 8
 POOL_SPLIT = 1
 WDS_POOL = False
 PRE_WD = False
-WARM_PASSES = 5
+WARM_PASSES = 3
 STEPS = [256] * 7 + [128, 128]
 
 
@@ -161,6 +169,10 @@ def tile_list_gmlpt_sigm_resL_kernel(
 
         residual = [keep.tile([P, 2, GATHER], F32, name="residual%d" % g, align_bytes=64) for g in range(J // GATHER)]
 
+        gathered = []
+        borrowed = []
+        lent = []
+
         def gate(j0):
             ga = project(psum_gate, 0, j0)
             ub = project(psum_up, 1, j0)
@@ -170,7 +182,7 @@ def tile_list_gmlpt_sigm_resL_kernel(
                 sig = residual[group][:, half, :]
             else:
                 sig = ring.tile([P, R], F32, name="sig")[:]
-            h_rows = ring.tile([P, 2, P, 2], BF16, name="h_rows", bufs=6)
+            h_rows = ring.tile([P, 2, P, 2], BF16, name="h_rows", bufs=H_ROWS)
             sig4 = sig.rearrange("j (u p e) -> j u p e", u=2, e=2)
             nc.scalar.activation(sig4, ga, SIGMOID)
             if tile in POOL:
@@ -184,11 +196,20 @@ def tile_list_gmlpt_sigm_resL_kernel(
                 for part in [slice(0, 1), slice(1, 2)] if j0 == J - P else [slice(0, 2)]:
                     nc.vector.tensor_tensor(h_rows[:, part], ub[:, part], sig4[:, part], MULT)
             if tile in PACE:
+                gathered.append((half, group))
                 nc.vector.tensor_copy(sig, res_table[half][:].indirect(listed(group * GATHER, GATHER)))
             return h_rows[:].rearrange("j u p e -> j (u p e)").bitcast(F32)
 
-        def turn(j0, rows):
-            turned = psum_turn.tile([P, len(rows), 2, P], F32, name="turned")
+        rows = {}
+
+        def turn(j0, width):
+            turn_rows(j0, [rows[s] for s in range(j0, j0 + width, P)])
+
+        def turn_rows(j0, rows):
+            if (j0, len(rows) * P) in borrowed:
+                turned = psum_gate.tile([P, len(rows), 2, P], F32, name="acc0")
+            else:
+                turned = psum_turn.tile([P, len(rows), 2, P], F32, name="turned")
             for s in range(len(rows)):
                 for u in range(2):
                     nc.tensor.transpose(turned[:, s, u, :], rows[s][:, u * P : (u + 1) * P], identity[:])
@@ -208,7 +229,10 @@ def tile_list_gmlpt_sigm_resL_kernel(
         outs = {}
 
         def down(j0, width):
-            y = psum_y.tile([P, 2, width], F32, name="y")
+            if (j0, width) in lent:
+                y = psum_up.tile([P, 2, width], F32, name="acc1")
+            else:
+                y = psum_y.tile([P, 2, width], F32, name="y")
             for half in range(2):
                 cols = slice(half * P, (half + 1) * P)
                 nc.tensor.matmul_mx(
@@ -230,6 +254,7 @@ def tile_list_gmlpt_sigm_resL_kernel(
         def finish(j0, width):
             fused = [h for h in range(2) if (h, j0 // GATHER) not in [PACE[t] for t in PACE]]
             picked_res = residual[j0 // GATHER][:, :, j0 % GATHER : j0 % GATHER + width]
+            assert all(h in fused or (h, j0 // GATHER) in gathered for h in range(2))
             if not fused:
                 result = ring.tile([P, 2, width], F32, name="result", bufs=6)
                 nc.vector.tensor_tensor(result[:], sums[j0][:], picked_res, ADD)
@@ -261,19 +286,32 @@ def tile_list_gmlpt_sigm_resL_kernel(
             lay_planes(1)
 
         starts = [sum(STEPS[:i]) for i in range(len(STEPS))]
-        rows = {}
-        for i in range(len(STEPS) + LAG_ADD):
-            if i < len(STEPS):
-                for s in range(starts[i], starts[i] + STEPS[i], P):
-                    if s % GATHER == 0:
-                        gather_last_pass(s)
-                    rows[s] = gate(s)
-            if 0 <= i - LAG_TURN < len(STEPS):
-                at = starts[i - LAG_TURN]
-                turn(at, [rows[s] for s in range(at, at + STEPS[i - LAG_TURN], P)])
-            if LAG_ADD > LAG_DOWN and 0 <= i - LAG_ADD < len(STEPS):
-                finish(starts[i - LAG_ADD], STEPS[i - LAG_ADD])
-            if 0 <= i - LAG_DOWN < len(STEPS):
-                down(starts[i - LAG_DOWN], STEPS[i - LAG_DOWN])
-            if LAG_ADD == LAG_DOWN and 0 <= i - LAG_ADD < len(STEPS):
-                finish(starts[i - LAG_ADD], STEPS[i - LAG_ADD])
+        tiles = J // P
+        stages = ((turn, LAG_TURN), (finish, LAG_ADD), (down, LAG_DOWN)) if LAG_ADD > LAG_DOWN else ((turn, LAG_TURN), (down, LAG_DOWN), (finish, LAG_ADD))
+
+        def due(at, width, lag):
+            last = (at + width) // P - 1
+            return (last | 3 if last < PAIRED_UPTO else last) + lag
+
+        for t in range(tiles):
+            if t * P % GATHER == 0:
+                gather_last_pass(t * P)
+            rows[t * P] = gate(t * P)
+            for stage, lag in stages:
+                for at, width in zip(starts, STEPS):
+                    if t == due(at, width, lag) and t < HOLD_FROM:
+                        stage(at, width)
+        late = [[(at, width) for at, width in zip(starts, STEPS) if due(at, width, lag) >= HOLD_FROM] for lag in (LAG_TURN, LAG_DOWN, LAG_ADD)]
+        borrowed.extend(late[0][len(late[0]) - BORROW_T :] if BORROW_T else [])
+        lent.extend(late[1][len(late[1]) - BORROW_Y :] if BORROW_Y else [])
+        if TAIL == "stages":
+            for stage, items in zip((turn, down, finish), late):
+                for at, width in items:
+                    stage(at, width)
+        else:
+            for at, width in zip(starts, STEPS):
+                for stage, items in zip((turn, down), late):
+                    if (at, width) in items:
+                        stage(at, width)
+            for at, width in late[2]:
+                finish(at, width)

@@ -23,25 +23,33 @@ PASSES = K // 512
 QUADS = 4
 GATHER = 512
 FIRST_PLANES = 1024
-POOL = [2, 3, 4, 5, 6, 7, 8, 9, 10, 11, 12]
-PACE = {2: (0, 0), 3: (0, 1), 4: (0, 2), 5: (0, 3), 6: (1, 0), 7: (1, 1), 8: (1, 2), 9: (1, 3)}
-LOADS = ["wu", "wg1", "res0", "wdw", "res1", "wds"]
+MID_PLANES = 1280
+POOL = [3, 4, 5, 6, 7]
+PACE = {1: (0, 2), 2: (0, 3), 3: (1, 2), 4: (1, 3)}
+LOADS = ["wg1", "wu", "wdw", "res0", "res1"]
 LATE_QUEUE = "gpsimd"
-BANKS = (2, 3, 1, 2)
+BANKS = (2, 3, 0, 3)
 LAST_BUFS = 3
 LAG_TURN = 2
 LAG_DOWN = 6
-LAG_ADD = 8
-PAIRED_UPTO = 8
+LAG_ADD = 12
+PAIRED_UPTO = 0
 HOLD_FROM = 16
-BORROW_T = 2
-BORROW_Y = 3
+FLIP_FROM = 16
+FLIP_SOONER = 1
+DIRECT_BUFS = 1
+Q_GATE = 99
+LAST_AFTER = {3: 0}
+POOL_ADDS = []
+ZERO_ON_POOL = True
+BORROW_T = 1
+BORROW_Y = 1
 TAIL = "stages"
 H_ROWS = 8
 POOL_SPLIT = 1
-WDS_POOL = False
+WDS_POOL = True
 PRE_WD = False
-WARM_PASSES = 3
+WARM_PASSES = 5
 STEPS = [256] * 7 + [128, 128]
 
 
@@ -54,7 +62,8 @@ def tile_list_gmlpt_sigm_resL_kernel(
         ring = ctx.enter_context(tc.tile_pool(name="ring", bufs=3))
         psum_gate = ctx.enter_context(tc.psum_pool(name="psum_gate", bufs=BANKS[0]))
         psum_up = ctx.enter_context(tc.psum_pool(name="psum_up", bufs=BANKS[1]))
-        psum_turn = ctx.enter_context(tc.psum_pool(name="psum_turn", bufs=BANKS[2]))
+        if BANKS[2]:
+            psum_turn = ctx.enter_context(tc.psum_pool(name="psum_turn", bufs=BANKS[2]))
         psum_y = ctx.enter_context(tc.psum_pool(name="psum_y", bufs=BANKS[3]))
 
         offsets = keep.tile([P, J // 16], U16, name="offsets")
@@ -63,13 +72,13 @@ def tile_list_gmlpt_sigm_resL_kernel(
         scale_table = keep.tile([P, T // 4], I32, name="scale_table", align_bytes=64)
         w_planes = [keep.tile([P, PASSES, R // 4], I32, name="w_plane%d" % m, align_bytes=64) for m in range(2)]
         wd_plane = keep.tile([P, N // 4], I32, name="wd_plane", align_bytes=64)
-        spans = ((0, FIRST_PLANES), (FIRST_PLANES, J))
+        spans = ((0, FIRST_PLANES), (FIRST_PLANES, MID_PLANES), (MID_PLANES, J)) if "mid" in LOADS else ((0, FIRST_PLANES), (FIRST_PLANES, J))
         planes = [keep.tile([P, PASSES, (b - a) // 4], I32, name="planes%d" % a, align_bytes=64) for a, b in spans]
         nc.gpsimd.memset(w_planes[0][:], 0)
         nc.vector.memset(w_planes[1][:], 0)
         nc.vector.memset(scale_table[:96, :], 0)
         for tile in (wd_plane, *planes):
-            nc.vector.memset(tile[:], 0)
+            (nc.gpsimd if ZERO_ON_POOL else nc.vector).memset(tile[:], 0)
 
         word_table = [keep.tile([P, T], I32, name="word_table%d" % a, align_bytes=64) for a in range(PASSES)]
         w_codes = [keep.tile([P, PASSES, R // 2], I32, name="w_codes%d" % m, align_bytes=64) for m in range(2)]
@@ -95,12 +104,32 @@ def tile_list_gmlpt_sigm_resL_kernel(
         identity = keep.tile([P, P], F32, name="identity")
         make_identity(nc, identity[:])
 
+        dealt_codes = [keep.tile([P, PASSES, 4, P, 2], U8, name="dealt_codes%d" % m, align_bytes=64) for m in range(2)]
+        dealt_planes = [keep.tile([P, PASSES, 4 * P], U8, name="dealt_planes%d" % m, align_bytes=64) for m in range(2)]
+
+        def deal_plane(m):
+            nc.gpsimd.tensor_copy(
+                dealt_planes[m][:].rearrange("p a (t q) -> p a t q", t=4),
+                w_planes[m][:].bitcast(U8).rearrange("p a (q t) -> p a t q", t=4),
+            )
+
+        def deal_codes(m, a):
+            nc.gpsimd.tensor_copy(
+                dealt_codes[m][:, a, :, :, :],
+                w_codes[m][:, a, :].bitcast(U8).rearrange("p (q t e) -> p t q e", t=4, e=2),
+            )
+
+        if FLIP_FROM < J // P:
+            deal_plane(0)
+            deal_codes(0, 0)
+            deal_plane(1)
+
         picked_scales = keep.tile([P, J], U8, name="picked_scales", align_bytes=64)
         nc.vector.tensor_copy(picked_scales[:], scale_table[:].bitcast(U8).indirect(offsets[:]))
 
         def lay_planes(part):
             for q in (0, 2, 1, 3):
-                (nc.sync, {"gpsimd": nc.gpsimd, "sync": nc.sync, "scalar": nc.scalar}[LATE_QUEUE])[part].dma_start(
+                (nc.sync if part < len(spans) - 1 else {"gpsimd": nc.gpsimd, "sync": nc.sync, "scalar": nc.scalar}[LATE_QUEUE]).dma_start(
                     planes[part][32 * q : 32 * q + 4, :, :], picked_scales[96 + 8 * q : 104 + 8 * q, spans[part][0] : spans[part][1]].bitcast(I32)
                 )
 
@@ -122,7 +151,7 @@ def tile_list_gmlpt_sigm_resL_kernel(
             if what in ("wd", "wds"):
                 for r in range(4):
                     nc.sync.dma_start(wd_plane[r:P:32, :], wd_scales[0, r:16:4, :].bitcast(I32))
-            if what == "late":
+            if what == "mid":
                 lay_planes(1)
 
         picked_first = keep.tile([P, J], U32, name="picked_first", align_bytes=64)
@@ -140,7 +169,10 @@ def tile_list_gmlpt_sigm_resL_kernel(
         picked_last = {}
 
         def gather_last_pass(j0):
-            picked_last[j0] = ring.tile([P, GATHER], U32, name="picked_last", bufs=LAST_BUFS, align_bytes=64)
+            if j0 // GATHER in LAST_AFTER:
+                picked_last[j0] = keep.tile([P, GATHER], U32, name="picked_late", tag="room%d" % LAST_AFTER[j0 // GATHER], align_bytes=64)
+            else:
+                picked_last[j0] = ring.tile([P, GATHER], U32, name="picked_last", bufs=LAST_BUFS, align_bytes=64)
             nc.vector.tensor_copy(picked_last[j0][:], word_table[1][:].bitcast(U32).indirect(listed(j0, GATHER)))
 
         def picked(a, j0):
@@ -149,9 +181,24 @@ def tile_list_gmlpt_sigm_resL_kernel(
             return picked_last[j0 - j0 % GATHER][:, j0 % GATHER : j0 % GATHER + P]
 
         def plane_of(a, j0):
-            late = j0 >= FIRST_PLANES
-            at = j0 - late * FIRST_PLANES
-            return planes[late][:, a, :].bitcast(U8)[:, at : at + P]
+            part = [k for k in range(len(spans)) if spans[k][0] <= j0][-1]
+            at = j0 - spans[part][0]
+            return planes[part][:, a, :].bitcast(U8)[:, at : at + P]
+
+        def project_flipped(pool, m, j0):
+            acc = pool.tile([P, 4, P], F32, name="acc%d" % m)
+            for t in range(4):
+                for a in range(PASSES):
+                    nc.tensor.matmul_mx(
+                        out=acc[:, t, :],
+                        lhsT=dealt_codes[m][:, a, t, :, :].rearrange("p q e -> p (q e)").bitcast(FP4X4),
+                        lhsT_scale=dealt_planes[m][:, a, t * P : (t + 1) * P],
+                        rhs=picked(a, j0).bitcast(FP8X4),
+                        rhs_scale=plane_of(a, j0),
+                        start=(a == 0),
+                        stop=(a == PASSES - 1),
+                    )
+            return acc[:].rearrange("p t j -> p j t")
 
         def project(pool, m, j0):
             acc = pool.tile([P, R], F32, name="acc%d" % m)
@@ -169,61 +216,89 @@ def tile_list_gmlpt_sigm_resL_kernel(
 
         residual = [keep.tile([P, 2, GATHER], F32, name="residual%d" % g, align_bytes=64) for g in range(J // GATHER)]
 
+        starts = [sum(STEPS[:i]) for i in range(len(STEPS))]
         gathered = []
         borrowed = []
         lent = []
 
+        h_of = {}
+        turned_steps = []
+
         def gate(j0):
-            ga = project(psum_gate, 0, j0)
-            ub = project(psum_up, 1, j0)
             tile = j0 // P
+            flipped = tile >= FLIP_FROM
+            ga = (project_flipped if flipped else project)(psum_gate, 0, j0)
+            ub = (project_flipped if flipped else project)(psum_up, 1, j0)
             if tile in PACE:
                 half, group = PACE[tile]
                 sig = residual[group][:, half, :]
+            elif tile in [LAST_AFTER[g] for g in LAST_AFTER]:
+                sig = keep.tile([P, R], F32, name="sig_room", tag="room%d" % tile, align_bytes=64)[:]
             else:
                 sig = ring.tile([P, R], F32, name="sig")[:]
-            h_rows = ring.tile([P, 2, P, 2], BF16, name="h_rows", bufs=H_ROWS)
-            sig4 = sig.rearrange("j (u p e) -> j u p e", u=2, e=2)
-            nc.scalar.activation(sig4, ga, SIGMOID)
+            if flipped:
+                if j0 in starts:
+                    h = ring.tile([P, STEPS[starts.index(j0)] // P, R], BF16, name="h_direct", bufs=DIRECT_BUFS, align_bytes=64)
+                    for s in range(STEPS[starts.index(j0)] // P):
+                        h_of[j0 + s * P] = (h, s)
+                rows = h_of[j0][0][:, h_of[j0][1], :]
+            elif tile in POOL and tile // 2 - Q_GATE in turned_steps:
+                turned_steps.remove(tile // 2 - Q_GATE)
+                rows = keep.tile([P, R], BF16, name="h_gated", tag="hq%d" % (tile // 2 - Q_GATE), align_bytes=64)[:]
+            else:
+                rows = ring.tile([P, R], BF16, name="h_rows", bufs=H_ROWS)[:]
+
+            def shaped(x):
+                if flipped:
+                    return x.rearrange("p (j t) -> p j t", t=4)
+                return x.rearrange("j (u p e) -> j u p e", u=2, e=2)
+
+            nc.scalar.activation(shaped(sig), ga, SIGMOID)
             if tile in POOL:
-                up = ring.tile([P, 2, P, 2], F32, name="up")
-                nc.scalar.copy(up[:], ub)
-                flat = [x.rearrange("j u p e -> j (u p e)") for x in (h_rows[:], up[:])]
+                up = ring.tile([P, R], F32, name="up")
+                nc.scalar.copy(shaped(up[:]), ub)
                 for k in range(POOL_SPLIT):
                     part = slice(k * R // POOL_SPLIT, (k + 1) * R // POOL_SPLIT)
-                    nc.gpsimd.tensor_tensor(flat[0][:, part], flat[1][:, part], sig[:, part], MULT)
+                    nc.gpsimd.tensor_tensor(rows[:, part], up[:, part], sig[:, part], MULT)
             else:
-                for part in [slice(0, 1), slice(1, 2)] if j0 == J - P else [slice(0, 2)]:
-                    nc.vector.tensor_tensor(h_rows[:, part], ub[:, part], sig4[:, part], MULT)
+                for part in [slice(0, 1), slice(1, 2)] if j0 == J - P and not flipped else [slice(0, P if flipped else 2)]:
+                    nc.vector.tensor_tensor(shaped(rows)[:, part], ub[:, part], shaped(sig)[:, part], MULT)
             if tile in PACE:
                 gathered.append((half, group))
                 nc.vector.tensor_copy(sig, res_table[half][:].indirect(listed(group * GATHER, GATHER)))
-            return h_rows[:].rearrange("j u p e -> j (u p e)").bitcast(F32)
+            return rows.bitcast(F32)
+
+        def quantize(j0, width, h):
+            nc.vector.quantize_mx(
+                out=h_codes[:, j0 : j0 + width].bitcast(FP8X4), scales=h_plane[:, j0 : j0 + width], in_=h
+            )
 
         rows = {}
 
         def turn(j0, width):
-            turn_rows(j0, [rows[s] for s in range(j0, j0 + width, P)])
+            if j0 // P >= FLIP_FROM:
+                quantize(j0, width, h_of[j0][0][:].rearrange("p s x -> p (s x)"))
+            else:
+                turn_rows(j0, [rows[s] for s in range(j0, j0 + width, P)])
 
         def turn_rows(j0, rows):
             if (j0, len(rows) * P) in borrowed:
                 turned = psum_gate.tile([P, len(rows), 2, P], F32, name="acc0")
+            elif BANKS[2] == 0:
+                turned = psum_y.tile([P, len(rows), 2, P], F32, name="y")
             else:
                 turned = psum_turn.tile([P, len(rows), 2, P], F32, name="turned")
             for s in range(len(rows)):
                 for u in range(2):
                     nc.tensor.transpose(turned[:, s, u, :], rows[s][:, u * P : (u + 1) * P], identity[:])
             width = len(rows) * P
-            h = ring.tile([P, width, 4], BF16, name="h", align_bytes=64)
+            h = keep.tile([P, width, 4], BF16, name="h", tag="hq%d" % starts.index(j0), align_bytes=64)
+            turned_steps.append(starts.index(j0))
             words = h[:].rearrange("p j t -> p (j t)").bitcast(F32)
             nc.scalar.copy(
                 words.rearrange("p (s j u) -> p s j u", j=P, u=2), turned[:].rearrange("p s u j -> p s j u")
             )
-            nc.vector.quantize_mx(
-                out=h_codes[:, j0 : j0 + width].bitcast(FP8X4),
-                scales=h_plane[:, j0 : j0 + width],
-                in_=h[:].rearrange("p n t -> p (n t)"),
-            )
+            quantize(j0, width, h[:].rearrange("p n t -> p (n t)"))
 
         sums = {}
         outs = {}
@@ -246,6 +321,10 @@ def tile_list_gmlpt_sigm_resL_kernel(
                 )
             sums[j0] = y
             fused = [h for h in range(2) if (h, j0 // GATHER) not in [PACE[t] for t in PACE]]
+            if not fused and starts.index(j0) in POOL_ADDS:
+                y_out = ring.tile([P, 2, width], F32, name="y_out", bufs=6)
+                nc.scalar.copy(y_out[:], y[:])
+                outs[j0] = y_out
             if fused:
                 y_out = ring.tile([P, 2, width], F32, name="y_out", bufs=6)
                 nc.scalar.copy(y_out[:, fused[0] : fused[-1] + 1, :], y[:, fused[0] : fused[-1] + 1, :])
@@ -257,7 +336,10 @@ def tile_list_gmlpt_sigm_resL_kernel(
             assert all(h in fused or (h, j0 // GATHER) in gathered for h in range(2))
             if not fused:
                 result = ring.tile([P, 2, width], F32, name="result", bufs=6)
-                nc.vector.tensor_tensor(result[:], sums[j0][:], picked_res, ADD)
+                if j0 in outs:
+                    nc.gpsimd.tensor_tensor(result[:], outs[j0][:], picked_res, ADD)
+                else:
+                    nc.vector.tensor_tensor(result[:], sums[j0][:], picked_res, ADD)
                 nc.sync.dma_start(out.rearrange("(h p) j -> p h j", h=2)[:, :, j0 : j0 + width], result[:])
                 return
             for half in range(2):
@@ -275,23 +357,25 @@ def tile_list_gmlpt_sigm_resL_kernel(
             nc.tensor.matmul_mx(
                 out=warm[:, :N] if PRE_WD else warm[:],
                 lhsT=picked_first[:, 0:P].bitcast(FP8X4),
-                lhsT_scale=plane_of(0, FIRST_PLANES),
+                lhsT_scale=plane_of(0, spans[-1][0]),
                 rhs=wd_codes[:].bitcast(FP8X4) if PRE_WD else w_codes[0][:, 0, :].bitcast(FP4X4),
                 rhs_scale=planes[1][:, 1, :N // 4].bitcast(U8) if PRE_WD else w_planes[0][:, 0, :].bitcast(U8),
                 start=True,
                 stop=True,
             )
 
-        if "late" not in LOADS:
-            lay_planes(1)
+        lay_planes(len(spans) - 1)
 
-        starts = [sum(STEPS[:i]) for i in range(len(STEPS))]
+        if FLIP_FROM < J // P:
+            for m, a in ((0, 1), (1, 0), (1, 1)):
+                deal_codes(m, a)
+
         tiles = J // P
         stages = ((turn, LAG_TURN), (finish, LAG_ADD), (down, LAG_DOWN)) if LAG_ADD > LAG_DOWN else ((turn, LAG_TURN), (down, LAG_DOWN), (finish, LAG_ADD))
 
         def due(at, width, lag):
             last = (at + width) // P - 1
-            return (last | 3 if last < PAIRED_UPTO else last) + lag
+            return (last | 3 if last < PAIRED_UPTO else last) + lag - (FLIP_SOONER if at // P >= FLIP_FROM else 0)
 
         for t in range(tiles):
             if t * P % GATHER == 0:

@@ -20,37 +20,22 @@ SIGMOID = mybir.ActivationFunctionType.Sigmoid
 
 P = 128
 PASSES = K // 512
-QUADS = 4
+HALVES = N // P
+SCALE_ROWS = 16
+SCALE_FROM = 96
 GATHER = 512
+FIRST_GATHER = 1024
 FIRST_PLANES = 1024
-MID_PLANES = 1280
-POOL = [3, 4, 5, 6, 7]
-PACE = {1: (0, 2), 2: (0, 3), 3: (1, 2), 4: (1, 3)}
-LOADS = ["wg1", "wu", "wdw", "res0", "res1"]
-LATE_QUEUE = "gpsimd"
-BANKS = (2, 3, 0, 3)
-LAST_BUFS = 3
-LAG_TURN = 2
-LAG_DOWN = 6
-LAG_ADD = 12
-PAIRED_UPTO = 0
-HOLD_FROM = 16
-FLIP_FROM = 16
-FLIP_SOONER = 1
-DIRECT_BUFS = 1
-Q_GATE = 99
-LAST_AFTER = {3: 0}
-POOL_ADDS = []
-ZERO_ON_POOL = True
-BORROW_T = 1
-BORROW_Y = 1
-TAIL = "stages"
-H_ROWS = 8
-POOL_SPLIT = 1
-WDS_POOL = True
-PRE_WD = False
 WARM_PASSES = 5
-STEPS = [256] * 7 + [128, 128]
+STEP = 2 * P
+STEPS = [STEP] * 7 + [P, P]
+AHEAD_FROM = 1024
+POOL_TILES = range(3, 8)
+DOWN_LAG = 3
+ADD_LAG = 6
+GATE_BANKS, UP_BANKS, SHARED_BANKS = 2, 3, 3
+ROW_BUFS = 8
+OUT_BUFS = 6
 
 
 def tile_list_gmlpt_sigm_resL_kernel(
@@ -60,11 +45,9 @@ def tile_list_gmlpt_sigm_resL_kernel(
     with ExitStack() as ctx:
         keep = ctx.enter_context(tc.tile_pool(name="keep", bufs=1))
         ring = ctx.enter_context(tc.tile_pool(name="ring", bufs=3))
-        psum_gate = ctx.enter_context(tc.psum_pool(name="psum_gate", bufs=BANKS[0]))
-        psum_up = ctx.enter_context(tc.psum_pool(name="psum_up", bufs=BANKS[1]))
-        if BANKS[2]:
-            psum_turn = ctx.enter_context(tc.psum_pool(name="psum_turn", bufs=BANKS[2]))
-        psum_y = ctx.enter_context(tc.psum_pool(name="psum_y", bufs=BANKS[3]))
+        psum_gate = ctx.enter_context(tc.psum_pool(name="psum_gate", bufs=GATE_BANKS))
+        psum_up = ctx.enter_context(tc.psum_pool(name="psum_up", bufs=UP_BANKS))
+        psum_shared = ctx.enter_context(tc.psum_pool(name="psum_shared", bufs=SHARED_BANKS))
 
         offsets = keep.tile([P, J // 16], U16, name="offsets")
         nc.sync.dma_start(offsets[:], offs)
@@ -72,108 +55,79 @@ def tile_list_gmlpt_sigm_resL_kernel(
         scale_table = keep.tile([P, T // 4], I32, name="scale_table", align_bytes=64)
         w_planes = [keep.tile([P, PASSES, R // 4], I32, name="w_plane%d" % m, align_bytes=64) for m in range(2)]
         wd_plane = keep.tile([P, N // 4], I32, name="wd_plane", align_bytes=64)
-        spans = ((0, FIRST_PLANES), (FIRST_PLANES, MID_PLANES), (MID_PLANES, J)) if "mid" in LOADS else ((0, FIRST_PLANES), (FIRST_PLANES, J))
+        spans = ((0, FIRST_PLANES), (FIRST_PLANES, J))
         planes = [keep.tile([P, PASSES, (b - a) // 4], I32, name="planes%d" % a, align_bytes=64) for a, b in spans]
         nc.gpsimd.memset(w_planes[0][:], 0)
         nc.vector.memset(w_planes[1][:], 0)
-        nc.vector.memset(scale_table[:96, :], 0)
+        nc.vector.memset(scale_table[:SCALE_FROM, :], 0)
         for tile in (wd_plane, *planes):
-            (nc.gpsimd if ZERO_ON_POOL else nc.vector).memset(tile[:], 0)
+            nc.gpsimd.memset(tile[:], 0)
 
         word_table = [keep.tile([P, T], I32, name="word_table%d" % a, align_bytes=64) for a in range(PASSES)]
         w_codes = [keep.tile([P, PASSES, R // 2], I32, name="w_codes%d" % m, align_bytes=64) for m in range(2)]
-        nc.sync.dma_start(scale_table[96:, :], tab_scales.bitcast(I32).rearrange("a q t -> q a t"))
-        nc.sync.dma_start(word_table[0][:], tab_words[0].rearrange("p t i -> p (t i)").bitcast(I32))
         wd_codes = keep.tile([P, N], I32, name="wd_codes", align_bytes=64)
-        if PRE_WD:
-            nc.sync.dma_start(wd_codes[:], wd_words[0].rearrange("p n i -> p (n i)").bitcast(I32))
-        else:
-            nc.sync.dma_start(w_codes[0][:, 0, :], wg_words[0].bitcast(I32))
+        nc.sync.dma_start(scale_table[SCALE_FROM:, :], tab_scales.bitcast(I32).rearrange("a q t -> q a t"))
+        nc.sync.dma_start(word_table[0][:], tab_words[0].rearrange("p t i -> p (t i)").bitcast(I32))
+        nc.sync.dma_start(w_codes[0][:, 0, :], wg_words[0].bitcast(I32))
         nc.sync.dma_start(word_table[1][:], tab_words[1].rearrange("p t i -> p (t i)").bitcast(I32))
 
         for m, (scales, queue) in enumerate(((wg_scales, nc.scalar), (wu_scales, nc.gpsimd))):
             for r in range(4):
                 queue.dma_start(
-                    w_planes[m][r:P:32, :, :], scales[:, r:16:4, :].bitcast(I32).rearrange("a q n -> q a n")
+                    w_planes[m][r:P:32, :, :], scales[:, r:SCALE_ROWS:4, :].bitcast(I32).rearrange("a q n -> q a n")
                 )
-
-        if WDS_POOL:
-            for r in range(4):
-                nc.gpsimd.dma_start(wd_plane[r:P:32, :], wd_scales[0, r:16:4, :].bitcast(I32))
+        for r in range(4):
+            nc.gpsimd.dma_start(wd_plane[r:P:32, :], wd_scales[0, r:SCALE_ROWS:4, :].bitcast(I32))
 
         identity = keep.tile([P, P], F32, name="identity")
         make_identity(nc, identity[:])
 
-        dealt_codes = [keep.tile([P, PASSES, 4, P, 2], U8, name="dealt_codes%d" % m, align_bytes=64) for m in range(2)]
-        dealt_planes = [keep.tile([P, PASSES, 4 * P], U8, name="dealt_planes%d" % m, align_bytes=64) for m in range(2)]
-
-        def deal_plane(m):
-            nc.gpsimd.tensor_copy(
-                dealt_planes[m][:].rearrange("p a (t q) -> p a t q", t=4),
-                w_planes[m][:].bitcast(U8).rearrange("p a (q t) -> p a t q", t=4),
-            )
-
-        def deal_codes(m, a):
-            nc.gpsimd.tensor_copy(
-                dealt_codes[m][:, a, :, :, :],
-                w_codes[m][:, a, :].bitcast(U8).rearrange("p (q t e) -> p t q e", t=4, e=2),
-            )
-
-        if FLIP_FROM < J // P:
-            deal_plane(0)
-            deal_codes(0, 0)
-            deal_plane(1)
-
         picked_scales = keep.tile([P, J], U8, name="picked_scales", align_bytes=64)
         nc.vector.tensor_copy(picked_scales[:], scale_table[:].bitcast(U8).indirect(offsets[:]))
 
-        def lay_planes(part):
-            for q in (0, 2, 1, 3):
-                (nc.sync if part < len(spans) - 1 else {"gpsimd": nc.gpsimd, "sync": nc.sync, "scalar": nc.scalar}[LATE_QUEUE]).dma_start(
-                    planes[part][32 * q : 32 * q + 4, :, :], picked_scales[96 + 8 * q : 104 + 8 * q, spans[part][0] : spans[part][1]].bitcast(I32)
+        def lay_planes(part, queue):
+            a, b = spans[part]
+            for quad in (0, 2, 1, 3):
+                rows_from = SCALE_FROM + 8 * quad
+                queue.dma_start(
+                    planes[part][32 * quad : 32 * quad + 4, :, :],
+                    picked_scales[rows_from : rows_from + 8, a:b].bitcast(I32),
                 )
 
-        lay_planes(0)
-        res_table = [keep.tile([P, T], F32, name="res_table%d" % half, align_bytes=64) for half in range(2)]
-        for what in LOADS:
-            if what == "wg1":
-                nc.sync.dma_start(w_codes[0][:, 1, :], wg_words[1].bitcast(I32))
-            if what == "wg":
-                nc.sync.dma_start(w_codes[0][:], wg_words.bitcast(I32).rearrange("a p n -> p a n"))
-            if what == "wu":
-                nc.sync.dma_start(w_codes[1][:], wu_words.bitcast(I32).rearrange("a p n -> p a n"))
-            if what in ("wu0", "wu1"):
-                nc.sync.dma_start(w_codes[1][:, int(what[2]), :], wu_words[int(what[2])].bitcast(I32))
-            if what in ("res0", "res1"):
-                nc.sync.dma_start(res_table[int(what[3])][:], rT[int(what[3]) * P : int(what[3]) * P + P, :])
-            if what in ("wd", "wdw"):
-                nc.sync.dma_start(wd_codes[:], wd_words[0].rearrange("p n i -> p (n i)").bitcast(I32))
-            if what in ("wd", "wds"):
-                for r in range(4):
-                    nc.sync.dma_start(wd_plane[r:P:32, :], wd_scales[0, r:16:4, :].bitcast(I32))
-            if what == "mid":
-                lay_planes(1)
-
-        picked_first = keep.tile([P, J], U32, name="picked_first", align_bytes=64)
-        h_codes = keep.tile([P, J], U32, name="h_codes", align_bytes=64)
-        h_plane = keep.tile([P, J], U8, name="h_plane", align_bytes=64)
+        lay_planes(0, nc.sync)
+        res_table = [keep.tile([P, T], F32, name="res_table%d" % half, align_bytes=64) for half in range(HALVES)]
+        nc.sync.dma_start(w_codes[0][:, 1, :], wg_words[1].bitcast(I32))
+        nc.sync.dma_start(w_codes[1][:], wu_words.bitcast(I32).rearrange("a p n -> p a n"))
+        nc.sync.dma_start(wd_codes[:], wd_words[0].rearrange("p n i -> p (n i)").bitcast(I32))
+        for half in range(HALVES):
+            nc.sync.dma_start(res_table[half][:], rT[half * P : (half + 1) * P, :])
 
         def listed(j0, width):
             return offsets[:, j0 // 16 : (j0 + width) // 16]
 
-        for j0, width in ((0, 1024), (1024, J - 1024)):
+        picked_first = keep.tile([P, J], U32, name="picked_first", align_bytes=64)
+        h_codes = keep.tile([P, J], U32, name="h_codes", align_bytes=64)
+        h_plane = keep.tile([P, J], U8, name="h_plane", align_bytes=64)
+        for j0 in range(0, J, FIRST_GATHER):
             nc.vector.tensor_copy(
-                picked_first[:, j0 : j0 + width], word_table[0][:].bitcast(U32).indirect(listed(j0, width))
+                picked_first[:, j0 : j0 + FIRST_GATHER],
+                word_table[0][:].bitcast(U32).indirect(listed(j0, FIRST_GATHER)),
             )
 
         picked_last = {}
 
         def gather_last_pass(j0):
-            if j0 // GATHER in LAST_AFTER:
-                picked_last[j0] = keep.tile([P, GATHER], U32, name="picked_late", tag="room%d" % LAST_AFTER[j0 // GATHER], align_bytes=64)
+            if j0 == J - GATHER:
+                picked_last[j0] = keep.tile([P, GATHER], U32, name="picked_late", tag="first_room", align_bytes=64)
             else:
-                picked_last[j0] = ring.tile([P, GATHER], U32, name="picked_last", bufs=LAST_BUFS, align_bytes=64)
+                picked_last[j0] = ring.tile([P, GATHER], U32, name="picked_last", align_bytes=64)
             nc.vector.tensor_copy(picked_last[j0][:], word_table[1][:].bitcast(U32).indirect(listed(j0, GATHER)))
+
+        residual = {
+            g0: keep.tile([P, HALVES, GATHER], F32, name="residual%d" % g0, align_bytes=64)
+            for g0 in range(AHEAD_FROM, J, GATHER)
+        }
+        ahead = [(half, g0) for half in range(HALVES) for g0 in residual]
 
         def picked(a, j0):
             if a == 0:
@@ -181,24 +135,9 @@ def tile_list_gmlpt_sigm_resL_kernel(
             return picked_last[j0 - j0 % GATHER][:, j0 % GATHER : j0 % GATHER + P]
 
         def plane_of(a, j0):
-            part = [k for k in range(len(spans)) if spans[k][0] <= j0][-1]
+            part = int(j0 >= FIRST_PLANES)
             at = j0 - spans[part][0]
             return planes[part][:, a, :].bitcast(U8)[:, at : at + P]
-
-        def project_flipped(pool, m, j0):
-            acc = pool.tile([P, 4, P], F32, name="acc%d" % m)
-            for t in range(4):
-                for a in range(PASSES):
-                    nc.tensor.matmul_mx(
-                        out=acc[:, t, :],
-                        lhsT=dealt_codes[m][:, a, t, :, :].rearrange("p q e -> p (q e)").bitcast(FP4X4),
-                        lhsT_scale=dealt_planes[m][:, a, t * P : (t + 1) * P],
-                        rhs=picked(a, j0).bitcast(FP8X4),
-                        rhs_scale=plane_of(a, j0),
-                        start=(a == 0),
-                        stop=(a == PASSES - 1),
-                    )
-            return acc[:].rearrange("p t j -> p j t")
 
         def project(pool, m, j0):
             acc = pool.tile([P, R], F32, name="acc%d" % m)
@@ -214,101 +153,64 @@ def tile_list_gmlpt_sigm_resL_kernel(
                 )
             return acc[:].rearrange("j (p u e) -> j u p e", u=2, e=2)
 
-        residual = [keep.tile([P, 2, GATHER], F32, name="residual%d" % g, align_bytes=64) for g in range(J // GATHER)]
+        def by_pairs(ap):
+            return ap.rearrange("j (u p e) -> j u p e", u=2, e=2)
 
-        starts = [sum(STEPS[:i]) for i in range(len(STEPS))]
-        gathered = []
-        borrowed = []
-        lent = []
-
-        h_of = {}
-        turned_steps = []
+        h_rows = {}
 
         def gate(j0):
             tile = j0 // P
-            flipped = tile >= FLIP_FROM
-            ga = (project_flipped if flipped else project)(psum_gate, 0, j0)
-            ub = (project_flipped if flipped else project)(psum_up, 1, j0)
-            if tile in PACE:
-                half, group = PACE[tile]
-                sig = residual[group][:, half, :]
-            elif tile in [LAST_AFTER[g] for g in LAST_AFTER]:
-                sig = keep.tile([P, R], F32, name="sig_room", tag="room%d" % tile, align_bytes=64)[:]
+            ga = project(psum_gate, 0, j0)
+            ub = project(psum_up, 1, j0)
+            paces = 1 <= tile <= len(ahead)
+            if paces:
+                half, g0 = ahead[tile - 1]
+                sig = residual[g0][:, half, :]
+            elif tile == 0:
+                sig = keep.tile([P, R], F32, name="sig_first", tag="first_room", align_bytes=64)[:]
             else:
                 sig = ring.tile([P, R], F32, name="sig")[:]
-            if flipped:
-                if j0 in starts:
-                    h = ring.tile([P, STEPS[starts.index(j0)] // P, R], BF16, name="h_direct", bufs=DIRECT_BUFS, align_bytes=64)
-                    for s in range(STEPS[starts.index(j0)] // P):
-                        h_of[j0 + s * P] = (h, s)
-                rows = h_of[j0][0][:, h_of[j0][1], :]
-            elif tile in POOL and tile // 2 - Q_GATE in turned_steps:
-                turned_steps.remove(tile // 2 - Q_GATE)
-                rows = keep.tile([P, R], BF16, name="h_gated", tag="hq%d" % (tile // 2 - Q_GATE), align_bytes=64)[:]
-            else:
-                rows = ring.tile([P, R], BF16, name="h_rows", bufs=H_ROWS)[:]
-
-            def shaped(x):
-                if flipped:
-                    return x.rearrange("p (j t) -> p j t", t=4)
-                return x.rearrange("j (u p e) -> j u p e", u=2, e=2)
-
-            nc.scalar.activation(shaped(sig), ga, SIGMOID)
-            if tile in POOL:
+            rows = ring.tile([P, R], BF16, name="rows", bufs=ROW_BUFS)[:]
+            nc.scalar.activation(by_pairs(sig), ga, SIGMOID)
+            if tile in POOL_TILES:
                 up = ring.tile([P, R], F32, name="up")
-                nc.scalar.copy(shaped(up[:]), ub)
-                for k in range(POOL_SPLIT):
-                    part = slice(k * R // POOL_SPLIT, (k + 1) * R // POOL_SPLIT)
-                    nc.gpsimd.tensor_tensor(rows[:, part], up[:, part], sig[:, part], MULT)
+                nc.scalar.copy(by_pairs(up[:]), ub)
+                nc.gpsimd.tensor_tensor(rows, up[:], sig, MULT)
             else:
-                for part in [slice(0, 1), slice(1, 2)] if j0 == J - P and not flipped else [slice(0, P if flipped else 2)]:
-                    nc.vector.tensor_tensor(shaped(rows)[:, part], ub[:, part], shaped(sig)[:, part], MULT)
-            if tile in PACE:
-                gathered.append((half, group))
-                nc.vector.tensor_copy(sig, res_table[half][:].indirect(listed(group * GATHER, GATHER)))
-            return rows.bitcast(F32)
-
-        def quantize(j0, width, h):
-            nc.vector.quantize_mx(
-                out=h_codes[:, j0 : j0 + width].bitcast(FP8X4), scales=h_plane[:, j0 : j0 + width], in_=h
-            )
-
-        rows = {}
+                for u in [slice(0, 1), slice(1, 2)] if j0 == J - P else [slice(0, 2)]:
+                    nc.vector.tensor_tensor(by_pairs(rows)[:, u], ub[:, u], by_pairs(sig)[:, u], MULT)
+            if paces:
+                nc.vector.tensor_copy(sig, res_table[half][:].indirect(listed(g0, GATHER)))
+            h_rows[j0] = rows.bitcast(F32)
 
         def turn(j0, width):
-            if j0 // P >= FLIP_FROM:
-                quantize(j0, width, h_of[j0][0][:].rearrange("p s x -> p (s x)"))
+            tiles = width // P
+            if j0 == J - P:
+                turned = psum_gate.tile([P, tiles, 2, P], F32, name="acc0")
             else:
-                turn_rows(j0, [rows[s] for s in range(j0, j0 + width, P)])
-
-        def turn_rows(j0, rows):
-            if (j0, len(rows) * P) in borrowed:
-                turned = psum_gate.tile([P, len(rows), 2, P], F32, name="acc0")
-            elif BANKS[2] == 0:
-                turned = psum_y.tile([P, len(rows), 2, P], F32, name="y")
-            else:
-                turned = psum_turn.tile([P, len(rows), 2, P], F32, name="turned")
-            for s in range(len(rows)):
+                turned = psum_shared.tile([P, tiles, 2, P], F32, name="shared")
+            for s in range(tiles):
                 for u in range(2):
-                    nc.tensor.transpose(turned[:, s, u, :], rows[s][:, u * P : (u + 1) * P], identity[:])
-            width = len(rows) * P
-            h = keep.tile([P, width, 4], BF16, name="h", tag="hq%d" % starts.index(j0), align_bytes=64)
-            turned_steps.append(starts.index(j0))
-            words = h[:].rearrange("p j t -> p (j t)").bitcast(F32)
+                    nc.tensor.transpose(turned[:, s, u, :], h_rows[j0 + s * P][:, u * P : (u + 1) * P], identity[:])
+            h = keep.tile([P, width, 4], BF16, name="h%d" % j0, align_bytes=64)
+            pairs = h[:].rearrange("p j t -> p (j t)").bitcast(F32)
             nc.scalar.copy(
-                words.rearrange("p (s j u) -> p s j u", j=P, u=2), turned[:].rearrange("p s u j -> p s j u")
+                pairs.rearrange("p (s j u) -> p s j u", j=P, u=2), turned[:].rearrange("p s u j -> p s j u")
             )
-            quantize(j0, width, h[:].rearrange("p n t -> p (n t)"))
+            nc.vector.quantize_mx(
+                out=h_codes[:, j0 : j0 + width].bitcast(FP8X4),
+                scales=h_plane[:, j0 : j0 + width],
+                in_=h[:].rearrange("p j t -> p (j t)"),
+            )
 
-        sums = {}
-        outs = {}
+        y_of = {}
 
         def down(j0, width):
-            if (j0, width) in lent:
-                y = psum_up.tile([P, 2, width], F32, name="acc1")
+            if j0 == J - P:
+                y = psum_up.tile([P, HALVES, width], F32, name="acc1")
             else:
-                y = psum_y.tile([P, 2, width], F32, name="y")
-            for half in range(2):
+                y = psum_shared.tile([P, HALVES, width], F32, name="shared")
+            for half in range(HALVES):
                 cols = slice(half * P, (half + 1) * P)
                 nc.tensor.matmul_mx(
                     out=y[:, half, :],
@@ -319,83 +221,48 @@ def tile_list_gmlpt_sigm_resL_kernel(
                     start=True,
                     stop=True,
                 )
-            sums[j0] = y
-            fused = [h for h in range(2) if (h, j0 // GATHER) not in [PACE[t] for t in PACE]]
-            if not fused and starts.index(j0) in POOL_ADDS:
-                y_out = ring.tile([P, 2, width], F32, name="y_out", bufs=6)
-                nc.scalar.copy(y_out[:], y[:])
-                outs[j0] = y_out
-            if fused:
-                y_out = ring.tile([P, 2, width], F32, name="y_out", bufs=6)
-                nc.scalar.copy(y_out[:, fused[0] : fused[-1] + 1, :], y[:, fused[0] : fused[-1] + 1, :])
-                outs[j0] = y_out
+            y_of[j0] = y
+            if j0 < AHEAD_FROM:
+                y_of[j0] = ring.tile([P, HALVES, width], F32, name="y_out", bufs=OUT_BUFS)
+                nc.scalar.copy(y_of[j0][:], y[:])
 
-        def finish(j0, width):
-            fused = [h for h in range(2) if (h, j0 // GATHER) not in [PACE[t] for t in PACE]]
-            picked_res = residual[j0 // GATHER][:, :, j0 % GATHER : j0 % GATHER + width]
-            assert all(h in fused or (h, j0 // GATHER) in gathered for h in range(2))
-            if not fused:
-                result = ring.tile([P, 2, width], F32, name="result", bufs=6)
-                if j0 in outs:
-                    nc.gpsimd.tensor_tensor(result[:], outs[j0][:], picked_res, ADD)
-                else:
-                    nc.vector.tensor_tensor(result[:], sums[j0][:], picked_res, ADD)
-                nc.sync.dma_start(out.rearrange("(h p) j -> p h j", h=2)[:, :, j0 : j0 + width], result[:])
-                return
-            for half in range(2):
-                result = ring.tile([P, width], F32, name="result", bufs=6)
-                if half in fused:
+        def add_residual(j0, width):
+            if j0 < AHEAD_FROM:
+                for half in range(HALVES):
+                    result = ring.tile([P, width], F32, name="result", bufs=OUT_BUFS)
                     nc.vector.tensor_tensor(
-                        result[:], res_table[half][:].indirect(listed(j0, width)), outs[j0][:, half, :], ADD
+                        result[:], res_table[half][:].indirect(listed(j0, width)), y_of[j0][:, half, :], ADD
                     )
-                else:
-                    nc.vector.tensor_tensor(result[:], sums[j0][:, half, :], picked_res[:, half, :], ADD)
-                nc.sync.dma_start(out[half * P : (half + 1) * P, j0 : j0 + width], result[:])
+                    nc.sync.dma_start(out[half * P : (half + 1) * P, j0 : j0 + width], result[:])
+            else:
+                at = j0 % GATHER
+                result = ring.tile([P, HALVES, width], F32, name="result", bufs=OUT_BUFS)
+                nc.vector.tensor_tensor(result[:], y_of[j0][:], residual[j0 - at][:, :, at : at + width], ADD)
+                nc.sync.dma_start(out.rearrange("(h p) j -> p h j", h=HALVES)[:, :, j0 : j0 + width], result[:])
 
-        warm = psum_y.tile([P, R], F32, name="y")
-        for i in range(WARM_PASSES):
+        warm = psum_shared.tile([P, R], F32, name="shared")
+        for _ in range(WARM_PASSES):
             nc.tensor.matmul_mx(
-                out=warm[:, :N] if PRE_WD else warm[:],
+                out=warm[:],
                 lhsT=picked_first[:, 0:P].bitcast(FP8X4),
-                lhsT_scale=plane_of(0, spans[-1][0]),
-                rhs=wd_codes[:].bitcast(FP8X4) if PRE_WD else w_codes[0][:, 0, :].bitcast(FP4X4),
-                rhs_scale=planes[1][:, 1, :N // 4].bitcast(U8) if PRE_WD else w_planes[0][:, 0, :].bitcast(U8),
+                lhsT_scale=plane_of(0, FIRST_PLANES),
+                rhs=w_codes[0][:, 0, :].bitcast(FP4X4),
+                rhs_scale=w_planes[0][:, 0, :].bitcast(U8),
                 start=True,
                 stop=True,
             )
+        lay_planes(1, nc.gpsimd)
 
-        lay_planes(len(spans) - 1)
-
-        if FLIP_FROM < J // P:
-            for m, a in ((0, 1), (1, 0), (1, 1)):
-                deal_codes(m, a)
-
-        tiles = J // P
-        stages = ((turn, LAG_TURN), (finish, LAG_ADD), (down, LAG_DOWN)) if LAG_ADD > LAG_DOWN else ((turn, LAG_TURN), (down, LAG_DOWN), (finish, LAG_ADD))
-
-        def due(at, width, lag):
-            last = (at + width) // P - 1
-            return (last | 3 if last < PAIRED_UPTO else last) + lag - (FLIP_SOONER if at // P >= FLIP_FROM else 0)
-
-        for t in range(tiles):
-            if t * P % GATHER == 0:
-                gather_last_pass(t * P)
-            rows[t * P] = gate(t * P)
-            for stage, lag in stages:
-                for at, width in zip(starts, STEPS):
-                    if t == due(at, width, lag) and t < HOLD_FROM:
-                        stage(at, width)
-        late = [[(at, width) for at, width in zip(starts, STEPS) if due(at, width, lag) >= HOLD_FROM] for lag in (LAG_TURN, LAG_DOWN, LAG_ADD)]
-        borrowed.extend(late[0][len(late[0]) - BORROW_T :] if BORROW_T else [])
-        lent.extend(late[1][len(late[1]) - BORROW_Y :] if BORROW_Y else [])
-        if TAIL == "stages":
-            for stage, items in zip((turn, down, finish), late):
-                for at, width in items:
-                    stage(at, width)
-        else:
-            for at, width in zip(starts, STEPS):
-                for stage, items in zip((turn, down), late):
-                    if (at, width) in items:
-                        stage(at, width)
-            for at, width in late[2]:
-                finish(at, width)
+        steps = [(sum(STEPS[:i]), STEPS[i]) for i in range(len(STEPS))]
+        rounds = J // STEP
+        for i in range(rounds):
+            if i * STEP % GATHER == 0:
+                gather_last_pass(i * STEP)
+            for j0 in range(i * STEP, (i + 1) * STEP, P):
+                gate(j0)
+            for stage, lag in ((turn, 1), (add_residual, ADD_LAG), (down, DOWN_LAG)):
+                if i >= lag:
+                    stage(*steps[i - lag])
+        for stage, lag in ((turn, 1), (down, DOWN_LAG), (add_residual, ADD_LAG)):
+            for j0, width in steps[rounds - lag :]:
+                stage(j0, width)

@@ -54,14 +54,13 @@ def tile_list_gmlpt_sigm_resL_kernel(
 
         scale_table = keep.tile([P, T // 4], I32, name="scale_table", align_bytes=64)
         w_planes = [keep.tile([P, PASSES, R // 4], I32, name="w_plane%d" % m, align_bytes=64) for m in range(2)]
-        wd_plane = keep.tile([P, N // 4], I32, name="wd_plane", align_bytes=64)
         spans = ((0, FIRST_PLANES), (FIRST_PLANES, J))
         planes = [keep.tile([P, PASSES, (b - a) // 4], I32, name="planes%d" % a, align_bytes=64) for a, b in spans]
         nc.gpsimd.memset(w_planes[0][:], 0)
         nc.vector.memset(w_planes[1][:], 0)
         nc.vector.memset(scale_table[:SCALE_FROM, :], 0)
-        for tile in (wd_plane, *planes):
-            nc.gpsimd.memset(tile[:], 0)
+        for tile in planes:
+            nc.vector.memset(tile[:], 0)
 
         word_table = [keep.tile([P, T], I32, name="word_table%d" % a, align_bytes=64) for a in range(PASSES)]
         w_codes = [keep.tile([P, PASSES, R // 2], I32, name="w_codes%d" % m, align_bytes=64) for m in range(2)]
@@ -76,14 +75,16 @@ def tile_list_gmlpt_sigm_resL_kernel(
                 queue.dma_start(
                     w_planes[m][r:P:32, :, :], scales[:, r:SCALE_ROWS:4, :].bitcast(I32).rearrange("a q n -> q a n")
                 )
-        for r in range(4):
-            nc.gpsimd.dma_start(wd_plane[r:P:32, :], wd_scales[0, r:SCALE_ROWS:4, :].bitcast(I32))
 
         identity = keep.tile([P, P], F32, name="identity")
         make_identity(nc, identity[:])
 
         picked_scales = keep.tile([P, J], U8, name="picked_scales", align_bytes=64)
         nc.vector.tensor_copy(picked_scales[:], scale_table[:].bitcast(U8).indirect(offsets[:]))
+
+        wd_plane = keep.tile([P, N // 4], I32, name="wd_plane", tag="scale_table", align_bytes=64)
+        for r in range(4):
+            nc.gpsimd.dma_start(wd_plane[r:P:32, :], wd_scales[0, r:SCALE_ROWS:4, :].bitcast(I32))
 
         def lay_planes(part, queue):
             a, b = spans[part]
@@ -121,7 +122,10 @@ def tile_list_gmlpt_sigm_resL_kernel(
                 picked_last[j0] = keep.tile([P, GATHER], U32, name="picked_late", tag="first_room", align_bytes=64)
             else:
                 picked_last[j0] = ring.tile([P, GATHER], U32, name="picked_last", align_bytes=64)
-            nc.vector.tensor_copy(picked_last[j0][:], word_table[1][:].bitcast(U32).indirect(listed(j0, GATHER)))
+            for at, width in [(0, STEP), (STEP, STEP)] if j0 == 0 else [(0, GATHER)]:
+                nc.vector.tensor_copy(
+                    picked_last[j0][:, at : at + width], word_table[1][:].bitcast(U32).indirect(listed(j0 + at, width))
+                )
 
         residual = {
             g0: keep.tile([P, HALVES, GATHER], F32, name="residual%d" % g0, align_bytes=64)

@@ -129,9 +129,10 @@ def tile_list_gmlpt_sigm_resL_kernel(
 
         residual = {
             g0: keep.tile([P, HALVES, GATHER], F32, name="residual%d" % g0, align_bytes=64)
-            for g0 in range(AHEAD_FROM, J, GATHER)
+            for g0 in range(AHEAD_FROM - GATHER, J, GATHER)
         }
-        ahead = [(half, g0) for half in range(HALVES) for g0 in residual]
+        late = range(AHEAD_FROM, J, GATHER)
+        ahead = [(0, g0) for g0 in late] + [(0, AHEAD_FROM - GATHER)] + [(1, g0) for g0 in late]
 
         def picked(a, j0):
             if a == 0:
@@ -234,9 +235,12 @@ def tile_list_gmlpt_sigm_resL_kernel(
             if j0 < AHEAD_FROM:
                 for half in range(HALVES):
                     result = ring.tile([P, width], F32, name="result", bufs=OUT_BUFS)
-                    nc.vector.tensor_tensor(
-                        result[:], res_table[half][:].indirect(listed(j0, width)), y_of[j0][:, half, :], ADD
-                    )
+                    at = j0 % GATHER
+                    if (half, j0 - at) in ahead:
+                        values = residual[j0 - at][:, half, at : at + width]
+                    else:
+                        values = res_table[half][:].indirect(listed(j0, width))
+                    nc.vector.tensor_tensor(result[:], values, y_of[j0][:, half, :], ADD)
                     nc.sync.dma_start(out[half * P : (half + 1) * P, j0 : j0 + width], result[:])
             else:
                 at = j0 % GATHER

@@ -31,6 +31,7 @@ STEP = 2 * P
 STEPS = [STEP] * 7 + [P, P]
 AHEAD_FROM = 1024
 POOL_TILES = range(3, 8)
+HELD = (STEP, 2 * STEP)
 DOWN_LAG = 3
 ADD_LAG = 6
 GATE_BANKS, UP_BANKS, SHARED_BANKS = 2, 3, 3
@@ -107,7 +108,6 @@ def tile_list_gmlpt_sigm_resL_kernel(
             return offsets[:, j0 // 16 : (j0 + width) // 16]
 
         picked_first = keep.tile([P, J], U32, name="picked_first", align_bytes=64)
-        h_codes = keep.tile([P, J], U32, name="h_codes", align_bytes=64)
         h_plane = keep.tile([P, J], U8, name="h_plane", align_bytes=64)
         for j0 in range(0, J, FIRST_GATHER):
             nc.vector.tensor_copy(
@@ -161,7 +161,8 @@ def tile_list_gmlpt_sigm_resL_kernel(
         def by_pairs(ap):
             return ap.rearrange("j (u p e) -> j u p e", u=2, e=2)
 
-        h_rows = {}
+        h_rows, h_codes = {}, {}
+        h_held = keep.tile([P, len(HELD) * STEP, 4], BF16, name="h_held", align_bytes=64)
 
         def gate(j0):
             tile = j0 // P
@@ -178,7 +179,10 @@ def tile_list_gmlpt_sigm_resL_kernel(
             rows = ring.tile([P, R], BF16, name="rows", bufs=ROW_BUFS)[:]
             nc.scalar.activation(by_pairs(sig), ga, SIGMOID)
             if tile in POOL_TILES:
-                up = ring.tile([P, R], F32, name="up")
+                if tile == POOL_TILES[-1]:
+                    up = keep.tile([P, R], F32, name="up_last", tag="last_up", align_bytes=64)
+                else:
+                    up = ring.tile([P, R], F32, name="up")
                 nc.scalar.copy(by_pairs(up[:]), ub)
                 nc.gpsimd.tensor_tensor(rows, up[:], sig, MULT)
             else:
@@ -197,16 +201,28 @@ def tile_list_gmlpt_sigm_resL_kernel(
             for s in range(tiles):
                 for u in range(2):
                     nc.tensor.transpose(turned[:, s, u, :], h_rows[j0 + s * P][:, u * P : (u + 1) * P], identity[:])
-            h = keep.tile([P, width, 4], BF16, name="h%d" % j0, align_bytes=64)
-            pairs = h[:].rearrange("p j t -> p (j t)").bitcast(F32)
+            if j0 in HELD:
+                h = h_held[:, j0 - HELD[0] : j0 - HELD[0] + width, :]
+            else:
+                h = keep.tile([P, width, 4], BF16, name="h%d" % j0, align_bytes=64)[:]
+            pairs = h.rearrange("p j t -> p (j t)").bitcast(F32)
             nc.scalar.copy(
                 pairs.rearrange("p (s j u) -> p s j u", j=P, u=2), turned[:].rearrange("p s u j -> p s j u")
             )
+            if j0 not in HELD:
+                h_codes[j0] = keep.tile([P, width], U32, name="h_codes%d" % j0, align_bytes=64)[:]
+                quantise(h_codes[j0], h, j0, width)
+
+        def quantise(codes, h, j0, width):
             nc.vector.quantize_mx(
-                out=h_codes[:, j0 : j0 + width].bitcast(FP8X4),
-                scales=h_plane[:, j0 : j0 + width],
-                in_=h[:].rearrange("p j t -> p (j t)"),
+                out=codes.bitcast(FP8X4), scales=h_plane[:, j0 : j0 + width], in_=h.rearrange("p j t -> p (j t)")
             )
+
+        def quantise_held():
+            codes = keep.tile([P, len(HELD) * STEP], U32, name="codes_held", tag="last_up", align_bytes=64)
+            quantise(codes[:], h_held[:], HELD[0], len(HELD) * STEP)
+            for j0 in HELD:
+                h_codes[j0] = codes[:, j0 - HELD[0] : j0 - HELD[0] + STEP]
 
         y_of = {}
 
@@ -221,7 +237,7 @@ def tile_list_gmlpt_sigm_resL_kernel(
                     out=y[:, half, :],
                     lhsT=wd_codes[:, cols].bitcast(FP8X4),
                     lhsT_scale=wd_plane[:].bitcast(U8)[:, cols],
-                    rhs=h_codes[:, j0 : j0 + width].bitcast(FP8X4),
+                    rhs=h_codes[j0].bitcast(FP8X4),
                     rhs_scale=h_plane[:, j0 : j0 + width],
                     start=True,
                     stop=True,
@@ -271,6 +287,8 @@ def tile_list_gmlpt_sigm_resL_kernel(
             for stage, lag in ((turn, 1), (add_residual, ADD_LAG), (down, DOWN_LAG)):
                 if i >= lag:
                     stage(*steps[i - lag])
+            if i == 3:
+                quantise_held()
         for stage, lag in ((turn, 1), (down, DOWN_LAG), (add_residual, ADD_LAG)):
             for j0, width in steps[rounds - lag :]:
                 stage(j0, width)

from contextlib import ExitStack

import concourse.mybir as mybir
from concourse.masks import make_identity

K, R, N, T, J = 1024, 512, 256, 4096, 2048
FLOPS = 2 * J * (2 * K * R + R * N)

F32 = mybir.dt.float32
BF16 = mybir.dt.bfloat16
I32 = mybir.dt.int32
U32 = mybir.dt.uint32
U16 = mybir.dt.uint16
U8 = mybir.dt.uint8
FP8X4 = mybir.dt.float8_e4m3fn_x4
FP4X4 = mybir.dt.float4_e2m1fn_x4
MULT = mybir.AluOpType.mult
ADD = mybir.AluOpType.add
SIGMOID = mybir.ActivationFunctionType.Sigmoid

P = 128
PASSES = K // 512
HALVES = N // P
SCALE_ROWS = 16
SCALE_FROM = 96
GATHER = 512
FIRST_GATHER = 1024
FIRST_PLANES = 1024
WARM_PASSES = 5
STEP = 2 * P
STEPS = [STEP] * 7 + [P, P]
AHEAD_FROM = 1024
POOL_TILES = range(3, 8)
HELD = (STEP, 2 * STEP)
DOWN_LAG = 3
ADD_LAG = 6
GATE_BANKS, UP_BANKS, SHARED_BANKS = 2, 3, 3
ROW_BUFS = 8
OUT_BUFS = 6


def tile_list_gmlpt_sigm_resL_kernel(
    tc, tab_words, tab_scales, wg_words, wg_scales, wu_words, wu_scales, wd_words, wd_scales, rT, offs, out
):
    nc = tc.nc
    with ExitStack() as ctx:
        keep = ctx.enter_context(tc.tile_pool(name="keep", bufs=1))
        ring = ctx.enter_context(tc.tile_pool(name="ring", bufs=3))
        psum_gate = ctx.enter_context(tc.psum_pool(name="psum_gate", bufs=GATE_BANKS))
        psum_up = ctx.enter_context(tc.psum_pool(name="psum_up", bufs=UP_BANKS))
        psum_shared = ctx.enter_context(tc.psum_pool(name="psum_shared", bufs=SHARED_BANKS))

        offsets = keep.tile([P, J // 16], U16, name="offsets")
        nc.sync.dma_start(offsets[:], offs)

        scale_table = keep.tile([P, T // 4], I32, name="scale_table", align_bytes=64)
        w_planes = [keep.tile([P, PASSES, R // 4], I32, name="w_plane%d" % m, align_bytes=64) for m in range(2)]
        spans = ((0, FIRST_PLANES), (FIRST_PLANES, J))
        planes = [keep.tile([P, PASSES, (b - a) // 4], I32, name="planes%d" % a, align_bytes=64) for a, b in spans]
        nc.gpsimd.memset(w_planes[0][:], 0)
        nc.vector.memset(w_planes[1][:], 0)
        nc.vector.memset(scale_table[:SCALE_FROM, :], 0)
        for tile in planes:
            nc.vector.memset(tile[:], 0)

        word_table = [keep.tile([P, T], I32, name="word_table%d" % a, align_bytes=64) for a in range(PASSES)]
        w_codes = [keep.tile([P, PASSES, R // 2], I32, name="w_codes%d" % m, align_bytes=64) for m in range(2)]
        wd_codes = keep.tile([P, N], I32, name="wd_codes", align_bytes=64)
        nc.sync.dma_start(scale_table[SCALE_FROM:, :], tab_scales.bitcast(I32).rearrange("a q t -> q a t"))
        nc.sync.dma_start(word_table[0][:], tab_words[0].rearrange("p t i -> p (t i)").bitcast(I32))
        nc.sync.dma_start(w_codes[0][:, 0, :], wg_words[0].bitcast(I32))
        nc.sync.dma_start(word_table[1][:], tab_words[1].rearrange("p t i -> p (t i)").bitcast(I32))

        for m, (scales, queue) in enumerate(((wg_scales, nc.scalar), (wu_scales, nc.gpsimd))):
            for r in range(4):
                queue.dma_start(
                    w_planes[m][r:P:32, :, :], scales[:, r:SCALE_ROWS:4, :].bitcast(I32).rearrange("a q n -> q a n")
                )

        identity = keep.tile([P, P], F32, name="identity")
        make_identity(nc, identity[:])

        picked_scales = keep.tile([P, J], U8, name="picked_scales", align_bytes=64)
        nc.vector.tensor_copy(picked_scales[:], scale_table[:].bitcast(U8).indirect(offsets[:]))

        wd_plane = keep.tile([P, N // 4], I32, name="wd_plane", tag="scale_table", align_bytes=64)
        for r in range(4):
            nc.gpsimd.dma_start(wd_plane[r:P:32, :], wd_scales[0, r:SCALE_ROWS:4, :].bitcast(I32))

        def lay_planes(part, queue):
            a, b = spans[part]
            for quad in (0, 2, 1, 3):
                rows_from = SCALE_FROM + 8 * quad
                queue.dma_start(
                    planes[part][32 * quad : 32 * quad + 4, :, :],
                    picked_scales[rows_from : rows_from + 8, a:b].bitcast(I32),
                )

        lay_planes(0, nc.sync)
        res_table = [keep.tile([P, T], F32, name="res_table%d" % half, align_bytes=64) for half in range(HALVES)]
        nc.sync.dma_start(w_codes[0][:, 1, :], wg_words[1].bitcast(I32))
        nc.sync.dma_start(w_codes[1][:], wu_words.bitcast(I32).rearrange("a p n -> p a n"))
        nc.sync.dma_start(wd_codes[:], wd_words[0].rearrange("p n i -> p (n i)").bitcast(I32))
        for half in range(HALVES):
            nc.sync.dma_start(res_table[half][:], rT[half * P : (half + 1) * P, :])

        def listed(j0, width):
            return offsets[:, j0 // 16 : (j0 + width) // 16]

        picked_first = keep.tile([P, J], U32, name="picked_first", align_bytes=64)
        h_plane = keep.tile([P, J], U8, name="h_plane", align_bytes=64)
        for j0 in range(0, J, FIRST_GATHER):
            nc.vector.tensor_copy(
                picked_first[:, j0 : j0 + FIRST_GATHER],
                word_table[0][:].bitcast(U32).indirect(listed(j0, FIRST_GATHER)),
            )

        picked_last = {}

        def gather_last_pass(j0):
            if j0 == J - GATHER:
                picked_last[j0] = keep.tile([P, GATHER], U32, name="picked_late", tag="first_room", align_bytes=64)
            else:
                picked_last[j0] = ring.tile([P, GATHER], U32, name="picked_last", align_bytes=64)
            for at, width in [(0, STEP), (STEP, STEP)] if j0 == 0 else [(0, GATHER)]:
                nc.vector.tensor_copy(
                    picked_last[j0][:, at : at + width], word_table[1][:].bitcast(U32).indirect(listed(j0 + at, width))
                )

        residual = {
            g0: keep.tile([P, HALVES, GATHER], F32, name="residual%d" % g0, align_bytes=64)
            for g0 in range(AHEAD_FROM - GATHER, J, GATHER)
        }
        late = range(AHEAD_FROM, J, GATHER)
        ahead = [(0, g0) for g0 in late] + [(0, AHEAD_FROM - GATHER)] + [(1, g0) for g0 in late]

        def picked(a, j0):
            if a == 0:
                return picked_first[:, j0 : j0 + P]
            return picked_last[j0 - j0 % GATHER][:, j0 % GATHER : j0 % GATHER + P]

        def plane_of(a, j0):
            part = int(j0 >= FIRST_PLANES)
            at = j0 - spans[part][0]
            return planes[part][:, a, :].bitcast(U8)[:, at : at + P]

        def project(pool, m, j0):
            acc = pool.tile([P, R], F32, name="acc%d" % m)
            for a in range(PASSES):
                nc.tensor.matmul_mx(
                    out=acc[:],
                    lhsT=picked(a, j0).bitcast(FP8X4),
                    lhsT_scale=plane_of(a, j0),
                    rhs=w_codes[m][:, a, :].bitcast(FP4X4),
                    rhs_scale=w_planes[m][:, a, :].bitcast(U8),
                    start=(a == 0),
                    stop=(a == PASSES - 1),
                )
            return acc[:].rearrange("j (p u e) -> j u p e", u=2, e=2)

        def by_pairs(ap):
            return ap.rearrange("j (u p e) -> j u p e", u=2, e=2)

        h_rows, h_codes = {}, {}
        h_held = keep.tile([P, len(HELD) * STEP, 4], BF16, name="h_held", align_bytes=64)

        def gate(j0):
            tile = j0 // P
            ga = project(psum_gate, 0, j0)
            ub = project(psum_up, 1, j0)
            paces = 1 <= tile <= len(ahead)
            if paces:
                half, g0 = ahead[tile - 1]
                sig = residual[g0][:, half, :]
            elif tile == 0:
                sig = keep.tile([P, R], F32, name="sig_first", tag="first_room", align_bytes=64)[:]
            else:
                sig = ring.tile([P, R], F32, name="sig")[:]
            rows = ring.tile([P, R], BF16, name="rows", bufs=ROW_BUFS)[:]
            nc.scalar.activation(by_pairs(sig), ga, SIGMOID)
            if tile in POOL_TILES:
                if tile == POOL_TILES[-1]:
                    up = keep.tile([P, R], F32, name="up_last", tag="last_up", align_bytes=64)
                else:
                    up = ring.tile([P, R], F32, name="up")
                nc.scalar.copy(by_pairs(up[:]), ub)
                nc.gpsimd.tensor_tensor(rows, up[:], sig, MULT)
            else:
                for u in [slice(0, 1), slice(1, 2)] if j0 == J - P else [slice(0, 2)]:
                    nc.vector.tensor_tensor(by_pairs(rows)[:, u], ub[:, u], by_pairs(sig)[:, u], MULT)
            if paces:
                nc.vector.tensor_copy(sig, res_table[half][:].indirect(listed(g0, GATHER)))
            h_rows[j0] = rows.bitcast(F32)

        def turn(j0, width):
            tiles = width // P
            if j0 == J - P:
                turned = psum_gate.tile([P, tiles, 2, P], F32, name="acc0")
            else:
                turned = psum_shared.tile([P, tiles, 2, P], F32, name="shared")
            for s in range(tiles):
                for u in range(2):
                    nc.tensor.transpose(turned[:, s, u, :], h_rows[j0 + s * P][:, u * P : (u + 1) * P], identity[:])
            if j0 in HELD:
                h = h_held[:, j0 - HELD[0] : j0 - HELD[0] + width, :]
            else:
                h = keep.tile([P, width, 4], BF16, name="h%d" % j0, align_bytes=64)[:]
            pairs = h.rearrange("p j t -> p (j t)").bitcast(F32)
            nc.scalar.copy(
                pairs.rearrange("p (s j u) -> p s j u", j=P, u=2), turned[:].rearrange("p s u j -> p s j u")
            )
            if j0 not in HELD:
                h_codes[j0] = keep.tile([P, width], U32, name="h_codes%d" % j0, align_bytes=64)[:]
                quantise(h_codes[j0], h, j0, width)

        def quantise(codes, h, j0, width):
            nc.vector.quantize_mx(
                out=codes.bitcast(FP8X4), scales=h_plane[:, j0 : j0 + width], in_=h.rearrange("p j t -> p (j t)")
            )

        def quantise_held():
            codes = keep.tile([P, len(HELD) * STEP], U32, name="codes_held", tag="last_up", align_bytes=64)
            quantise(codes[:], h_held[:], HELD[0], len(HELD) * STEP)
            for j0 in HELD:
                h_codes[j0] = codes[:, j0 - HELD[0] : j0 - HELD[0] + STEP]

        y_of = {}

        def down(j0, width):
            if j0 == J - P:
                y = psum_up.tile([P, HALVES, width], F32, name="acc1")
            else:
                y = psum_shared.tile([P, HALVES, width], F32, name="shared")
            for half in range(HALVES):
                cols = slice(half * P, (half + 1) * P)
                nc.tensor.matmul_mx(
                    out=y[:, half, :],
                    lhsT=wd_codes[:, cols].bitcast(FP8X4),
                    lhsT_scale=wd_plane[:].bitcast(U8)[:, cols],
                    rhs=h_codes[j0].bitcast(FP8X4),
                    rhs_scale=h_plane[:, j0 : j0 + width],
                    start=True,
                    stop=True,
                )
            y_of[j0] = y
            if j0 < AHEAD_FROM:
                y_of[j0] = ring.tile([P, HALVES, width], F32, name="y_out", bufs=OUT_BUFS)
                nc.scalar.copy(y_of[j0][:], y[:])

        def add_residual(j0, width):
            if j0 < AHEAD_FROM:
                for half in range(HALVES):
                    result = ring.tile([P, width], F32, name="result", bufs=OUT_BUFS)
                    at = j0 % GATHER
                    if (half, j0 - at) in ahead:
                        values = residual[j0 - at][:, half, at : at + width]
                    else:
                        values = res_table[half][:].indirect(listed(j0, width))
                    nc.vector.tensor_tensor(result[:], values, y_of[j0][:, half, :], ADD)
                    nc.sync.dma_start(out[half * P : (half + 1) * P, j0 : j0 + width], result[:])
            else:
                at = j0 % GATHER
                result = ring.tile([P, HALVES, width], F32, name="result", bufs=OUT_BUFS)
                nc.vector.tensor_tensor(result[:], y_of[j0][:], residual[j0 - at][:, :, at : at + width], ADD)
                nc.sync.dma_start(out.rearrange("(h p) j -> p h j", h=HALVES)[:, :, j0 : j0 + width], result[:])

        warm = psum_shared.tile([P, R], F32, name="shared")
        for _ in range(WARM_PASSES):
            nc.tensor.matmul_mx(
                out=warm[:],
                lhsT=picked_first[:, 0:P].bitcast(FP8X4),
                lhsT_scale=plane_of(0, FIRST_PLANES),
                rhs=w_codes[0][:, 0, :].bitcast(FP4X4),
                rhs_scale=w_planes[0][:, 0, :].bitcast(U8),
                start=True,
                stop=True,
            )
        lay_planes(1, nc.gpsimd)

        steps = [(sum(STEPS[:i]), STEPS[i]) for i in range(len(STEPS))]
        rounds = J // STEP
        for i in range(rounds):
            if i * STEP % GATHER == 0:
                gather_last_pass(i * STEP)
            for j0 in range(i * STEP, (i + 1) * STEP, P):
                gate(j0)
            for stage, lag in ((turn, 1), (add_residual, ADD_LAG), (down, DOWN_LAG)):
                if i >= lag:
                    stage(*steps[i - lag])
            if i == 3:
                quantise_held()
        for stage, lag in ((turn, 1), (down, DOWN_LAG), (add_residual, ADD_LAG)):
            for j0, width in steps[rounds - lag :]:
                stage(j0, width)
